import numpy as np
import ml_dtypes


def mxq(x, axis, fmt="e4m3"):
    dtype, down = {"e4m3": (ml_dtypes.float8_e4m3fn, 7), "e5m2": (ml_dtypes.float8_e5m2, 14)}[fmt]
    v = np.moveaxis(np.asarray(x, np.float32).astype(ml_dtypes.bfloat16).astype(np.float64), axis, -1)
    blocks = v.reshape(v.shape[:-1] + (-1, 32))
    amax = np.abs(blocks).max(-1, keepdims=True)
    byte = np.maximum(np.where(amax > 0, np.frexp(amax)[1] - 1 + 127, 0) - down, 1)
    scale = np.exp2(byte - 127.0)
    codes = (blocks / scale).astype(np.float32).astype(dtype).astype(np.float64)
    return np.moveaxis((codes * scale).reshape(v.shape), -1, axis)


WIDE = False


def mx_kscale(k):
    if not WIDE:
        return np.ones(k)
    levels = np.array([10, -10, 5, -5, 0])
    if k % 512:
        return np.exp2(np.random.permutation(np.resize(levels, k // 32))).repeat(32)
    a = np.empty((k // 512, 16))
    for p in range(k // 512):
        a[p, :8] = np.random.permutation(np.resize(levels, 8))
        for g in range(8):
            far = levels[np.abs(levels - a[p, g]) >= 10]
            a[p, g + 8] = far[np.random.randint(len(far))]
    return np.exp2(a.ravel()).repeat(32)


def f64(x):
    return np.asarray(x).astype(np.float64)


def striped(idx):
    return np.tile(idx.reshape(-1, 16).T, (8, 1)).astype(np.uint16)


def unstriped(offs):
    return offs[:16].T.reshape(-1).astype(np.int64)


E2M1 = np.array([0.0, 0.5, 1.0, 1.5, 2.0, 3.0, 4.0, 6.0, -0.0, -0.5, -1.0, -1.5, -2.0, -3.0, -4.0, -6.0])


def pack_weight(w, fmt):
    k, n = w.shape
    w = f64(np.asarray(w, np.float32).astype(ml_dtypes.bfloat16)).reshape(k // 32, 32, n)
    amax = np.abs(w).max(1)
    if fmt == "e4m3":
        byte = np.frexp(amax)[1] - 1 + 127 - 7
    else:
        mant, ex = np.frexp(amax / 6.0)
        byte = np.where(mant > 0.5, ex, ex - 1) + 127
    byte = np.clip(np.where(amax > 0, byte, 1), 1, 254)
    scaled = (w * np.exp2(127.0 - byte)[:, None, :]).reshape(k, n).astype(np.float32)
    by_word = np.ascontiguousarray(scaled.reshape(k // 512, 128, 4, n).transpose(0, 1, 3, 2))
    if fmt == "e4m3":
        words = by_word.astype(ml_dtypes.float8_e4m3fn).view(np.uint8)
    else:
        c = by_word.astype(ml_dtypes.float4_e2m1fn).view(np.uint8) & 0xF
        words = (c[..., 0::2] | (c[..., 1::2] << 4)).reshape(k // 512, 128, 2 * n)
    return np.ascontiguousarray(words), np.ascontiguousarray(byte.astype(np.uint8).reshape(k // 512, 16, n))


def unpack_weight(words, scales, fmt):
    g, _, n = scales.shape
    words = np.ascontiguousarray(words).reshape(g, 128, n, -1)
    if fmt == "e4m3":
        vals = words.view(ml_dtypes.float8_e4m3fn).astype(np.float64)
    else:
        nib = np.empty((g, 128, n, 4), np.uint8)
        nib[..., 0::2] = words & 0xF
        nib[..., 1::2] = words >> 4
        vals = E2M1[nib]
    vals = vals * np.repeat(np.exp2(scales.astype(np.float64) - 127.0), 8, axis=1)[..., None]
    return vals.transpose(0, 1, 3, 2).reshape(g * 512, n)


def gelu(v):
    return 0.5 * v * (1.0 + np.tanh(np.sqrt(2.0 / np.pi) * (v + 0.044715 * v**3)))


def striped8(idx):
    return np.concatenate([v.reshape(-1, 16).T for v in idx]).astype(np.uint16)


def unstriped8(offs):
    return np.stack([offs[16 * g:16 * g + 16].T.reshape(-1) for g in range(8)]).astype(np.int64)


def heads(h, wgt, idx8):
    r = np.arange(h.shape[0])
    return wgt[r // 4 % 128] * h[r[:, None], idx8[r % 512 // 64]]


T, S, P, K, D, H, N = 2048, 1024, 512, 512, 512, 1536, 512

def setup_inputs():
    n = np.random.standard_normal
    s = mx_kscale(K)[:, None]
    d = mx_kscale(D)[:, None]
    u = mx_kscale(H)[:, None]
    tab_words, tab_scales = pack_weight(n((K, T)) * s, "e4m3")
    wr_words, wr_scales = pack_weight(n((K, H)) / np.sqrt(K) / s * u.T, "e2m1")
    wf_words, wf_scales = pack_weight(n((H, N)) / np.sqrt(H) / u, "e4m3")
    return {
        "tab_words": tab_words, "tab_scales": tab_scales,
        "offs": striped(np.random.permutation(T)[:S]),
        "wr_words": wr_words, "wr_scales": wr_scales,
        "offs2": striped8(np.stack([np.random.permutation(S)[:P] for _ in range(8)])),
        "wgt": np.repeat(np.random.uniform(0.5, 2.0, (8, P)), 16, axis=0).astype(np.float32),
        "tf": (n((D, P)) * d).astype(np.float32),
        "wt": (0.36 * n((D, H)) / np.sqrt(D) / d).astype(np.float32),
        "phase": np.random.uniform(-0.9, 0.9, H).astype(np.float32),
        "wf_words": wf_words, "wf_scales": wf_scales,
        "bf": (0.5 * n(N)).astype(np.float32),
        "sev": np.exp(0.3 * n(N)).astype(np.float32),
    }

def reference(tab_words, tab_scales, offs, wr_words, wr_scales, offs2, wgt, tf, wt, phase,
              wf_words, wf_scales, bf, sev):
    v = unpack_weight(tab_words, tab_scales, "e4m3")[:, unstriped(offs)]
    h = unpack_weight(wr_words, wr_scales, "e2m1").T @ v
    x = heads(h, f64(wgt), unstriped8(offs2))
    a = mxq(f64(wt), 0, "e4m3").T @ mxq(f64(tf), 0, "e4m3")
    z = x * np.cos(a + f64(phase)[:, None])
    y = unpack_weight(wf_words, wf_scales, "e4m3").T @ mxq(z, 0, "e4m3")
    return f64(sev)[:, None] / (1.0 + np.exp(-(y + f64(bf)[:, None])))

@@ -1,0 +1,214 @@
+import math
+from contextlib import ExitStack
+
+import concourse.mybir as mybir
+
+T, S, M, H, N = 2048, 1024, 512, 1536, 512
+FLOPS = 2 * 512 * H * S + 2 * 512 * H * M + 2 * H * N * M
+
+F32 = mybir.dt.float32
+BF16 = mybir.dt.bfloat16
+I32 = mybir.dt.int32
+U32 = mybir.dt.uint32
+U16 = mybir.dt.uint16
+U8 = mybir.dt.uint8
+FP8X4 = mybir.dt.float8_e4m3fn_x4
+FP4X4 = mybir.dt.float4_e2m1fn_x4
+ACT = mybir.ActivationFunctionType
+ALU = mybir.AluOpType
+
+P = 128
+PACK = 4
+BLOCKS = H // (P * PACK)
+BANK = 512
+HALF = M // 2
+
+
+def tile_list_event_graph_forecast_kernel(
+    tc, tab_words, tab_scales, offs, wr_words, wr_scales, offs2, wgt, tf, wt, phase,
+    wf_words, wf_scales, bf, sev, out,
+):
+    nc = tc.nc
+    with ExitStack() as ctx:
+        keep = ctx.enter_context(tc.tile_pool(name="keep", bufs=1))
+        loads = ctx.enter_context(tc.tile_pool(name="loads", bufs=1))
+        ring = ctx.enter_context(tc.tile_pool(name="ring", bufs=2))
+        psum = ctx.enter_context(tc.psum_pool(name="psum", bufs=4))
+
+        idx = keep.tile([P, S // 16], U16, name="idx")
+        idx2 = keep.tile([P, M // 16], U16, name="idx2")
+        tab_w = loads.tile([P, T], U32, name="tab_w", align_bytes=64, offset=0)
+        tab_s = keep.tile([P, T], U8, name="tab_s", align_bytes=64)
+        wr_w = loads.tile([P, 2 * H], U8, name="wr_w", align_bytes=64, offset=8192)
+        wr_s = keep.tile([P, H], U8, name="wr_s", align_bytes=64)
+        wf_w = loads.tile([P, BLOCKS, N], U32, name="wf_w", align_bytes=64, offset=12288)
+        wf_s = keep.tile([P, BLOCKS, N], U8, name="wf_s", align_bytes=64)
+        wgt_sb = loads.tile([P, M], F32, name="wgt_sb", offset=18432)
+        phase_sb = loads.tile([P, BLOCKS, PACK], F32, name="phase_sb", offset=20480)
+        bf_sb = loads.tile([P, N // P], F32, name="bf_sb", offset=20544)
+        sev_sb = loads.tile([P, N // P], F32, name="sev_sb", offset=20608)
+        half_bf = keep.tile([P, N // P], F32, name="half_bf")
+        half_sev = keep.tile([P, N // P], F32, name="half_sev")
+        one = loads.tile([P, 3072], F32, name="one", offset=0)
+        pi = loads.tile([P, 11264], F32, name="pi", offset=12288)
+        half_pi = keep.tile([P, 1], F32, name="half_pi")
+        warm = keep.tile([P, 1], F32, name="warm")
+
+        nc.gpsimd.memset(tab_s[:].bitcast(I32), 0)
+        nc.vector.memset(one[:, 0:1], 1.0)
+        nc.vector.tensor_scalar(pi[:, 0:1], one[:, 0:1], math.pi, None, ALU.mult)
+        nc.vector.memset(wr_s[:].bitcast(I32), 0)
+        nc.vector.tensor_scalar(half_pi[:], pi[:, 0:1], 0.5, None, ALU.mult)
+        nc.scalar.activation(out=warm[:], in_=half_pi[:], func=ACT.Silu)
+        nc.vector.memset(wf_s[:].rearrange("p a c -> p (a c)").bitcast(I32), 0)
+
+        nc.sync.dma_start(idx[:], offs)
+        for q in range(4):
+            nc.sync.dma_start(tab_s[32 * q : 32 * q + 4, :].bitcast(I32), tab_scales[0, 4 * q : 4 * q + 4, :].bitcast(I32))
+        nc.sync.dma_start(tab_w[:].bitcast(I32), tab_words[0].rearrange("p t i -> p (t i)").bitcast(I32))
+        nc.sync.dma_start(wr_w[:].bitcast(I32), wr_words[0].bitcast(I32))
+        for q in range(4):
+            nc.sync.dma_start(wr_s[32 * q : 32 * q + 4, :].bitcast(I32), wr_scales[0, 4 * q : 4 * q + 4, :].bitcast(I32))
+        nc.sync.dma_start(idx2[:], offs2)
+
+        tf_raw = loads.tile([P, PACK, M], F32, name="tf_raw", offset=24576)
+        nc.sync.dma_start(tf_raw[:], tf.rearrange("(p j) m -> p j m", j=PACK))
+        wt_raw = []
+        for b in range(BLOCKS):
+            raw = loads.tile([P, PACK, BANK], F32, name="wt_raw%d" % b, offset=32768 + 8192 * b)
+            nc.sync.dma_start(raw[:], wt[:, BANK * b : BANK * (b + 1)].rearrange("(p j) c -> p j c", j=PACK))
+            wt_raw.append(raw)
+            if b == 0:
+                nc.sync.dma_start(wgt_sb[:], wgt)
+                nc.sync.dma_start(phase_sb[:], phase.rearrange("(b p i) -> p b i", b=BLOCKS, i=PACK))
+        nc.sync.dma_start(
+            wf_w[:].bitcast(I32), wf_words.rearrange("a p c i -> p a (c i)").bitcast(I32))
+        for q in range(4):
+            nc.sync.dma_start(
+                wf_s[32 * q : 32 * q + 4, :, :].bitcast(I32),
+                wf_scales[:, 4 * q : 4 * q + 4, :].rearrange("a r c -> r a c").bitcast(I32))
+        with nc.allow_non_contiguous_dma(reason="one value a partition"):
+            nc.sync.dma_start(bf_sb[:], bf.rearrange("(u p) -> p u", p=P))
+            nc.sync.dma_start(sev_sb[:], sev.rearrange("(u p) -> p u", p=P))
+
+        def permute_wr(b):
+            words = keep.tile([P, 2 * BANK], U8, name="wr_wp%d" % b, align_bytes=64)
+            scales = keep.tile([P, BANK], U8, name="wr_sp%d" % b, align_bytes=64)
+            nc.vector.tensor_copy(
+                words[:].bitcast(U16).rearrange("p (t c e) -> p c t e", t=PACK, e=8),
+                wr_w[:, 2 * BANK * b : 2 * BANK * (b + 1)].bitcast(U16).rearrange("p (c e t) -> p c t e", t=PACK, e=8))
+            nc.vector.tensor_copy(
+                scales[:].rearrange("p (t c e) -> p c t e", t=PACK, e=16),
+                wr_s[:, BANK * b : BANK * (b + 1)].rearrange("p (c e t) -> p c t e", t=PACK, e=16))
+            return words, scales
+
+        def gather_table(window, dtype, name, half):
+            picked = keep.tile([P, BANK], dtype, name="%s%d" % (name, half), align_bytes=64)
+            nc.vector.tensor_copy(picked[:], window[:].indirect(idx[:, 32 * half : 32 * (half + 1)]))
+            return picked
+
+        def quantise(grouped, name):
+            codes = keep.tile([P, BANK], U32, name=name + "_codes", align_bytes=64)
+            scales = keep.tile([P, BANK], U8, name=name + "_scales", align_bytes=64)
+            nc.vector.quantize_mx(out=codes[:].bitcast(FP8X4), scales=scales[:], in_=grouped[:])
+            return codes, scales
+
+        def group_wt(b, engine_copy):
+            grouped = ring.tile([P, PACK * BANK], BF16, name="wt_grouped", align_bytes=64)
+            engine_copy(
+                grouped[:].rearrange("p (t c j) -> p c j t", t=PACK, j=PACK),
+                wt_raw[b][:].rearrange("p j (c t) -> p c j t", t=PACK))
+            return grouped
+
+        def project(b, wr_p, v):
+            planes = [keep.tile([P, S], F32, name="h%d_%d" % (b, t)) for t in range(PACK)]
+            for t in range(PACK):
+                for half in range(2):
+                    acc = psum.tile([P, BANK], F32, name="acc")
+                    nc.tensor.matmul_mx(
+                        out=acc[:], lhsT=wr_p[0][:, 2 * P * t : 2 * P * (t + 1)].bitcast(FP4X4),
+                        lhsT_scale=wr_p[1][:, P * t : P * (t + 1)],
+                        rhs=v[half][0][:].bitcast(FP8X4), rhs_scale=v[half][1][:], start=True, stop=True)
+                    nc.scalar.copy(planes[t][:, BANK * half : BANK * (half + 1)], acc[:])
+            return planes
+
+        def angles(b, wt_q, tf_q):
+            size = ring.tile([P, PACK, M], F32, name="size")
+            for t in range(PACK):
+                acc = psum.tile([P, BANK], F32, name="acc")
+                nc.tensor.matmul_mx(
+                    out=acc[:], lhsT=wt_q[0][:, P * t : P * (t + 1)].bitcast(FP8X4),
+                    lhsT_scale=wt_q[1][:, P * t : P * (t + 1)],
+                    rhs=tf_q[0][:].bitcast(FP8X4), rhs_scale=tf_q[1][:], start=True, stop=True)
+                nc.scalar.activation(out=size[:, t, :], in_=acc[:], func=ACT.Abs, bias=phase_sb[:, b, t : t + 1])
+            cos = ring.tile([P, PACK, M], F32, name="cos")
+            nc.scalar.activation(out=cos[:], in_=size[:], func=ACT.Sin, bias=half_pi[:], scale=-1.0)
+            return cos
+
+        def modulate(b, planes, cos, lo, width):
+            x = ring.tile([P, PACK, width], F32, name="x")
+            for t in range(PACK):
+                nc.vector.tensor_tensor(
+                    x[:, t, :], planes[t][:].indirect(idx2[:, lo // 16 : (lo + width) // 16]),
+                    wgt_sb[:, lo : lo + width], ALU.mult)
+            z = ring.tile([P, PACK * width], BF16, name="z", align_bytes=64)
+            nc.vector.tensor_tensor(
+                z[:].rearrange("p (c e t) -> p c t e", t=PACK, e=2),
+                x[:].rearrange("p t (c e) -> p c t e", e=2),
+                cos[:, :, lo : lo + width].rearrange("p t (c e) -> p c t e", e=2), ALU.mult)
+            codes = keep.tile([P, width], U32, name="z_codes%d_%d" % (b, lo), align_bytes=64)
+            scales = keep.tile([P, width], U8, name="z_scales%d_%d" % (b, lo), align_bytes=64)
+            nc.vector.quantize_mx(out=codes[:].bitcast(FP8X4), scales=scales[:], in_=z[:])
+            return codes, scales
+
+        def forecast_pass(acc, u, b, codes, scales):
+            nc.tensor.matmul_mx(
+                out=acc, lhsT=wf_w[:, b, P * u : P * (u + 1)].bitcast(FP8X4),
+                lhsT_scale=wf_s[:, b, P * u : P * (u + 1)],
+                rhs=codes.bitcast(FP8X4), rhs_scale=scales, start=(b == 0), stop=(b == BLOCKS - 1))
+
+        v_s = [gather_table(tab_s, U8, "v_s", half) for half in range(2)]
+        wr_p = permute_wr(0)
+        v = [(gather_table(tab_w, U32, "v_w", half), v_s[half]) for half in range(2)]
+        planes = project(0, wr_p, v)
+
+        tf_grouped = ring.tile([P, PACK * M], BF16, name="wt_grouped", align_bytes=64)
+        nc.vector.tensor_copy(
+            tf_grouped[:].rearrange("p (c e j) -> p c j e", j=PACK, e=4),
+            tf_raw[:].rearrange("p j (c e) -> p c j e", e=4))
+        wt_grouped = group_wt(0, nc.vector.tensor_copy)
+        tf_q = quantise(tf_grouped, "tf")
+        wt_q = quantise(wt_grouped, "wt0")
+        nc.scalar.mul(half_bf[:], bf_sb[:], 0.5)
+        nc.scalar.mul(half_sev[:], sev_sb[:], 0.5)
+
+        z_q = []
+        for b in range(BLOCKS):
+            cos = angles(b, wt_q, tf_q)
+            if b + 1 < BLOCKS:
+                wt_grouped = group_wt(b + 1, nc.scalar.copy if b else nc.vector.tensor_copy)
+                wr_p = permute_wr(b + 1)
+                next_planes = project(b + 1, wr_p, v)
+                z_q.append(modulate(b, planes, cos, 0, M))
+                wt_q = quantise(wt_grouped, "wt%d" % (b + 1))
+                planes = next_planes
+
+        last = BLOCKS - 1
+        for half in range(2):
+            lo = HALF * half
+            accs = [psum.tile([P, HALF], F32, name="y%d_%d" % (half, u), tag="acc" if half else "y") for u in range(N // P)]
+            for u in range(N // P):
+                for b in range(last):
+                    forecast_pass(accs[u][:], u, b, z_q[b][0][:, lo : lo + HALF], z_q[b][1][:, lo : lo + HALF])
+            codes, scales = modulate(last, planes, cos, lo, HALF)
+            for u in range(N // P):
+                forecast_pass(accs[u][:], u, last, codes[:], scales[:])
+                tanh = ring.tile([P, HALF], F32, name="tanh", bufs=4)
+                nc.scalar.activation(out=tanh[:], in_=accs[u][:], func=ACT.Tanh, bias=half_bf[:, u : u + 1], scale=0.5)
+                res = ring.tile([P, HALF], F32, name="res", bufs=8)
+                if half == 0:
+                    nc.scalar.activation(out=res[:], in_=tanh[:], func=ACT.Identity,
+                                         bias=half_sev[:, u : u + 1], scale=half_sev[:, u : u + 1])
+                else:
+                    nc.vector.tensor_scalar(res[:], tanh[:], half_sev[:, u : u + 1], half_sev[:, u : u + 1], ALU.mult, ALU.add)
+                nc.sync.dma_start(out[P * u : P * (u + 1), lo : lo + HALF], res[:])

@@ -70,6 +70,7 @@ def tile_list_event_graph_forecast_kernel(
         for q in range(4):
             nc.sync.dma_start(wr_s[32 * q : 32 * q + 4, :].bitcast(I32), wr_scales[0, 4 * q : 4 * q + 4, :].bitcast(I32))
         nc.sync.dma_start(idx2[:], offs2)
+        nc.sync.dma_start(wgt_sb[:], wgt)
 
         tf_raw = loads.tile([P, PACK, M], F32, name="tf_raw", offset=24576)
         nc.sync.dma_start(tf_raw[:], tf.rearrange("(p j) m -> p j m", j=PACK))
@@ -79,7 +80,6 @@ def tile_list_event_graph_forecast_kernel(
             nc.sync.dma_start(raw[:], wt[:, BANK * b : BANK * (b + 1)].rearrange("(p j) c -> p j c", j=PACK))
             wt_raw.append(raw)
             if b == 0:
-                nc.sync.dma_start(wgt_sb[:], wgt)
                 nc.sync.dma_start(phase_sb[:], phase.rearrange("(b p i) -> p b i", b=BLOCKS, i=PACK))
         nc.sync.dma_start(
             wf_w[:].bitcast(I32), wf_words.rearrange("a p c i -> p a (c i)").bitcast(I32))
@@ -116,8 +116,8 @@ def tile_list_event_graph_forecast_kernel(
         def group_wt(b, engine_copy):
             grouped = ring.tile([P, PACK * BANK], BF16, name="wt_grouped", align_bytes=64)
             engine_copy(
-                grouped[:].rearrange("p (t c j) -> p c j t", t=PACK, j=PACK),
-                wt_raw[b][:].rearrange("p j (c t) -> p c j t", t=PACK))
+                grouped[:].rearrange("p (t c j) -> p c t j", t=PACK, j=PACK),
+                wt_raw[b][:].rearrange("p j (c t) -> p c t j", t=PACK))
             return grouped
 
         def project(b, wr_p, v):
@@ -132,7 +132,7 @@ def tile_list_event_graph_forecast_kernel(
                     nc.scalar.copy(planes[t][:, BANK * half : BANK * (half + 1)], acc[:])
             return planes
 
-        def angles(b, wt_q, tf_q):
+        def magnitudes(b, wt_q, tf_q):
             size = ring.tile([P, PACK, M], F32, name="size")
             for t in range(PACK):
                 acc = psum.tile([P, BANK], F32, name="acc")
@@ -141,21 +141,22 @@ def tile_list_event_graph_forecast_kernel(
                     lhsT_scale=wt_q[1][:, P * t : P * (t + 1)],
                     rhs=tf_q[0][:].bitcast(FP8X4), rhs_scale=tf_q[1][:], start=True, stop=True)
                 nc.scalar.activation(out=size[:, t, :], in_=acc[:], func=ACT.Abs, bias=phase_sb[:, b, t : t + 1])
-            cos = ring.tile([P, PACK, M], F32, name="cos")
-            nc.scalar.activation(out=cos[:], in_=size[:], func=ACT.Sin, bias=half_pi[:], scale=-1.0)
-            return cos
+            return size
 
-        def modulate(b, planes, cos, lo, width):
-            x = ring.tile([P, PACK, width], F32, name="x")
+        def pick(b, planes):
+            x = keep.tile([P, PACK, M], F32, name="x%d" % b)
             for t in range(PACK):
-                nc.vector.tensor_tensor(
-                    x[:, t, :], planes[t][:].indirect(idx2[:, lo // 16 : (lo + width) // 16]),
-                    wgt_sb[:, lo : lo + width], ALU.mult)
+                nc.vector.tensor_tensor(x[:, t, :], planes[t][:].indirect(idx2[:]), wgt_sb[:], ALU.mult)
+            return x
+
+        def modulate(b, x, size, lo, width):
+            cos = ring.tile([P, PACK, width], F32, name="cos")
+            nc.scalar.activation(out=cos[:], in_=size[:, :, lo : lo + width], func=ACT.Sin, bias=half_pi[:], scale=-1.0)
             z = ring.tile([P, PACK * width], BF16, name="z", align_bytes=64)
             nc.vector.tensor_tensor(
                 z[:].rearrange("p (c e t) -> p c t e", t=PACK, e=2),
-                x[:].rearrange("p t (c e) -> p c t e", e=2),
-                cos[:, :, lo : lo + width].rearrange("p t (c e) -> p c t e", e=2), ALU.mult)
+                x[:, :, lo : lo + width].rearrange("p t (c e) -> p c t e", e=2),
+                cos[:].rearrange("p t (c e) -> p c t e", e=2), ALU.mult)
             codes = keep.tile([P, width], U32, name="z_codes%d_%d" % (b, lo), align_bytes=64)
             scales = keep.tile([P, width], U8, name="z_scales%d_%d" % (b, lo), align_bytes=64)
             nc.vector.quantize_mx(out=codes[:].bitcast(FP8X4), scales=scales[:], in_=z[:])
@@ -168,47 +169,36 @@ def tile_list_event_graph_forecast_kernel(
                 rhs=codes.bitcast(FP8X4), rhs_scale=scales, start=(b == 0), stop=(b == BLOCKS - 1))
 
         v_s = [gather_table(tab_s, U8, "v_s", half) for half in range(2)]
-        wr_p = permute_wr(0)
+        wr_p = [permute_wr(0)]
         v = [(gather_table(tab_w, U32, "v_w", half), v_s[half]) for half in range(2)]
-        planes = project(0, wr_p, v)
+        wr_p.extend(permute_wr(b) for b in range(1, BLOCKS))
+        planes = [project(b, wr_p[b], v) for b in range(BLOCKS)]
 
         tf_grouped = ring.tile([P, PACK * M], BF16, name="wt_grouped", align_bytes=64)
         nc.vector.tensor_copy(
             tf_grouped[:].rearrange("p (c e j) -> p c j e", j=PACK, e=4),
             tf_raw[:].rearrange("p j (c e) -> p c j e", e=4))
-        wt_grouped = group_wt(0, nc.vector.tensor_copy)
+        last = BLOCKS - 1
         tf_q = quantise(tf_grouped, "tf")
-        wt_q = quantise(wt_grouped, "wt0")
+        wt_q = [quantise(group_wt(b, nc.scalar.copy if b == last else nc.vector.tensor_copy), "wt%d" % b) for b in range(BLOCKS)]
+        x = [pick(b, planes[b]) for b in range(BLOCKS)]
         nc.scalar.mul(half_bf[:], bf_sb[:], 0.5)
         nc.scalar.mul(half_sev[:], sev_sb[:], 0.5)
 
-        z_q = []
-        for b in range(BLOCKS):
-            cos = angles(b, wt_q, tf_q)
-            if b + 1 < BLOCKS:
-                wt_grouped = group_wt(b + 1, nc.scalar.copy if b else nc.vector.tensor_copy)
-                wr_p = permute_wr(b + 1)
-                next_planes = project(b + 1, wr_p, v)
-                z_q.append(modulate(b, planes, cos, 0, M))
-                wt_q = quantise(wt_grouped, "wt%d" % (b + 1))
-                planes = next_planes
-
-        last = BLOCKS - 1
+        z_q = [modulate(b, x[b], magnitudes(b, wt_q[b], tf_q), 0, M) for b in range(last)]
+        size = magnitudes(last, wt_q[last], tf_q)
+        z_last = [modulate(last, x[last], size, HALF * half, HALF) for half in range(2)]
         for half in range(2):
             lo = HALF * half
             accs = [psum.tile([P, HALF], F32, name="y%d_%d" % (half, u), tag="acc" if half else "y") for u in range(N // P)]
             for u in range(N // P):
                 for b in range(last):
                     forecast_pass(accs[u][:], u, b, z_q[b][0][:, lo : lo + HALF], z_q[b][1][:, lo : lo + HALF])
-            codes, scales = modulate(last, planes, cos, lo, HALF)
+            codes, scales = z_last[half]
             for u in range(N // P):
                 forecast_pass(accs[u][:], u, last, codes[:], scales[:])
-                tanh = ring.tile([P, HALF], F32, name="tanh", bufs=4)
+                tanh = ring.tile([P, HALF], F32, name="tanh", bufs=8)
                 nc.scalar.activation(out=tanh[:], in_=accs[u][:], func=ACT.Tanh, bias=half_bf[:, u : u + 1], scale=0.5)
                 res = ring.tile([P, HALF], F32, name="res", bufs=8)
-                if half == 0:
-                    nc.scalar.activation(out=res[:], in_=tanh[:], func=ACT.Identity,
-                                         bias=half_sev[:, u : u + 1], scale=half_sev[:, u : u + 1])
-                else:
-                    nc.vector.tensor_scalar(res[:], tanh[:], half_sev[:, u : u + 1], half_sev[:, u : u + 1], ALU.mult, ALU.add)
+                nc.vector.tensor_scalar(res[:], tanh[:], half_sev[:, u : u + 1], half_sev[:, u : u + 1], ALU.mult, ALU.add)
                 nc.sync.dma_start(out[P * u : P * (u + 1), lo : lo + HALF], res[:])

@@ -22,6 +22,7 @@ PACK = 4
 BLOCKS = H // (P * PACK)
 BANK = 512
 HALF = M // 2
+QUARTER = M // 4
 
 
 def tile_list_event_graph_forecast_kernel(
@@ -60,7 +61,7 @@ def tile_list_event_graph_forecast_kernel(
         nc.vector.memset(wr_s[:].bitcast(I32), 0)
         nc.vector.tensor_scalar(half_pi[:], pi[:, 0:1], 0.5, None, ALU.mult)
         nc.scalar.activation(out=warm[:], in_=half_pi[:], func=ACT.Silu)
-        nc.vector.memset(wf_s[:].rearrange("p a c -> p (a c)").bitcast(I32), 0)
+        nc.gpsimd.memset(wf_s[:].rearrange("p a c -> p (a c)").bitcast(I32), 0)
 
         nc.sync.dma_start(idx[:], offs)
         for q in range(4):
@@ -113,11 +114,14 @@ def tile_list_event_graph_forecast_kernel(
             nc.vector.quantize_mx(out=codes[:].bitcast(FP8X4), scales=scales[:], in_=grouped[:])
             return codes, scales
 
-        def group_wt(b, engine_copy):
+        def group_wt(b, on_scalar):
             grouped = ring.tile([P, PACK * BANK], BF16, name="wt_grouped", align_bytes=64)
-            engine_copy(
-                grouped[:].rearrange("p (t c j) -> p c t j", t=PACK, j=PACK),
-                wt_raw[b][:].rearrange("p j (c t) -> p c t j", t=PACK))
+            dst = grouped[:].rearrange("p (t c j) -> p c t j", t=PACK, j=PACK)
+            src = wt_raw[b][:].rearrange("p j (c t) -> p c t j", t=PACK)
+            if on_scalar:
+                nc.scalar.copy(dst, src)
+            else:
+                nc.vector.tensor_copy(dst, src)
             return grouped
 
         def project(b, wr_p, v):
@@ -149,14 +153,17 @@ def tile_list_event_graph_forecast_kernel(
                 nc.vector.tensor_tensor(x[:, t, :], planes[t][:].indirect(idx2[:]), wgt_sb[:], ALU.mult)
             return x
 
-        def modulate(b, x, size, lo, width):
-            cos = ring.tile([P, PACK, width], F32, name="cos")
+        def cosine(size, lo, width):
+            cos = ring.tile([P, PACK, width], F32, name="cos%d" % width, bufs=2 if width == M else 4)
             nc.scalar.activation(out=cos[:], in_=size[:, :, lo : lo + width], func=ACT.Sin, bias=half_pi[:], scale=-1.0)
-            z = ring.tile([P, PACK * width], BF16, name="z", align_bytes=64)
+            return cos
+
+        def modulate(b, x, cos, lo, width):
+            z = ring.tile([P, PACK * width], BF16, name="z%d" % width, align_bytes=64, bufs=2 if width == M else 4)
             nc.vector.tensor_tensor(
                 z[:].rearrange("p (c e t) -> p c t e", t=PACK, e=2),
                 x[:, :, lo : lo + width].rearrange("p t (c e) -> p c t e", e=2),
-                cos[:].rearrange("p t (c e) -> p c t e", e=2), ALU.mult)
+                cos.rearrange("p t (c e) -> p c t e", e=2), ALU.mult)
             codes = keep.tile([P, width], U32, name="z_codes%d_%d" % (b, lo), align_bytes=64)
             scales = keep.tile([P, width], U8, name="z_scales%d_%d" % (b, lo), align_bytes=64)
             nc.vector.quantize_mx(out=codes[:].bitcast(FP8X4), scales=scales[:], in_=z[:])
@@ -180,25 +187,30 @@ def tile_list_event_graph_forecast_kernel(
             tf_raw[:].rearrange("p j (c e) -> p c j e", e=4))
         last = BLOCKS - 1
         tf_q = quantise(tf_grouped, "tf")
-        wt_q = [quantise(group_wt(b, nc.scalar.copy if b == last else nc.vector.tensor_copy), "wt%d" % b) for b in range(BLOCKS)]
+        wt_q = [quantise(group_wt(b, b == last), "wt%d" % b) for b in range(BLOCKS)]
         x = [pick(b, planes[b]) for b in range(BLOCKS)]
         nc.scalar.mul(half_bf[:], bf_sb[:], 0.5)
         nc.scalar.mul(half_sev[:], sev_sb[:], 0.5)
 
-        z_q = [modulate(b, x[b], magnitudes(b, wt_q[b], tf_q), 0, M) for b in range(last)]
+        z_q = [modulate(b, x[b], cosine(magnitudes(b, wt_q[b], tf_q), 0, M)[:], 0, M) for b in range(last)]
         size = magnitudes(last, wt_q[last], tf_q)
-        z_last = [modulate(last, x[last], size, HALF * half, HALF) for half in range(2)]
-        for half in range(2):
-            lo = HALF * half
-            accs = [psum.tile([P, HALF], F32, name="y%d_%d" % (half, u), tag="acc" if half else "y") for u in range(N // P)]
-            for u in range(N // P):
+        z_last = [modulate(last, x[last], cosine(size, lo, QUARTER)[:], lo, QUARTER) for lo in range(0, M, QUARTER)]
+
+        types = N // P
+        out_v = out.rearrange("(u p) m -> p u m", p=P)
+        for piece in range(M // QUARTER):
+            cols = slice(QUARTER * piece, QUARTER * (piece + 1))
+            accs = [psum.tile([P, QUARTER], F32, name="y%d_%d" % (piece, u), tag="acc" if piece % 2 else "y") for u in range(types)]
+            for u in range(types):
                 for b in range(last):
-                    forecast_pass(accs[u][:], u, b, z_q[b][0][:, lo : lo + HALF], z_q[b][1][:, lo : lo + HALF])
-            codes, scales = z_last[half]
-            for u in range(N // P):
-                forecast_pass(accs[u][:], u, last, codes[:], scales[:])
-                tanh = ring.tile([P, HALF], F32, name="tanh", bufs=8)
-                nc.scalar.activation(out=tanh[:], in_=accs[u][:], func=ACT.Tanh, bias=half_bf[:, u : u + 1], scale=0.5)
-                res = ring.tile([P, HALF], F32, name="res", bufs=8)
-                nc.vector.tensor_scalar(res[:], tanh[:], half_sev[:, u : u + 1], half_sev[:, u : u + 1], ALU.mult, ALU.add)
-                nc.sync.dma_start(out[P * u : P * (u + 1), lo : lo + HALF], res[:])
+                    forecast_pass(accs[u][:], u, b, z_q[b][0][:, cols], z_q[b][1][:, cols])
+            for u in range(types):
+                forecast_pass(accs[u][:], u, last, z_last[piece][0][:], z_last[piece][1][:])
+            group = 2 if piece == M // QUARTER - 1 else types
+            for first in range(0, types, group):
+                res = ring.tile([P, group, QUARTER], F32, name="res", bufs=5)
+                for u in range(first, first + group):
+                    tanh = ring.tile([P, QUARTER], F32, name="tanh", bufs=16)
+                    nc.scalar.activation(out=tanh[:], in_=accs[u][:], func=ACT.Tanh, bias=half_bf[:, u : u + 1], scale=0.5)
+                    nc.vector.tensor_scalar(res[:, u - first, :], tanh[:], half_sev[:, u : u + 1], half_sev[:, u : u + 1], ALU.mult, ALU.add)
+                nc.sync.dma_start(out_v[:, first : first + group, cols], res[:])

@@ -23,6 +23,7 @@ BLOCKS = H // (P * PACK)
 BANK = 512
 HALF = M // 2
 QUARTER = M // 4
+PIECES = [(0, HALF), (HALF, QUARTER), (HALF + QUARTER, QUARTER)]
 
 
 def tile_list_event_graph_forecast_kernel(
@@ -33,184 +34,217 @@ def tile_list_event_graph_forecast_kernel(
     with ExitStack() as ctx:
         keep = ctx.enter_context(tc.tile_pool(name="keep", bufs=1))
         loads = ctx.enter_context(tc.tile_pool(name="loads", bufs=1))
-        ring = ctx.enter_context(tc.tile_pool(name="ring", bufs=2))
         psum = ctx.enter_context(tc.psum_pool(name="psum", bufs=4))
 
         idx = keep.tile([P, S // 16], U16, name="idx")
         idx2 = keep.tile([P, M // 16], U16, name="idx2")
-        tab_w = loads.tile([P, T], U32, name="tab_w", align_bytes=64, offset=0)
         tab_s = keep.tile([P, T], U8, name="tab_s", align_bytes=64)
-        wr_w = loads.tile([P, 2 * H], U8, name="wr_w", align_bytes=64, offset=8192)
-        wr_s = keep.tile([P, H], U8, name="wr_s", align_bytes=64)
-        wf_w = loads.tile([P, BLOCKS, N], U32, name="wf_w", align_bytes=64, offset=12288)
+        wr_s = loads.tile([P, H], U8, name="wr_s", align_bytes=64, offset=57344)
         wf_s = keep.tile([P, BLOCKS, N], U8, name="wf_s", align_bytes=64)
+        half_bf = keep.tile([P, N // P], F32, name="half_bf")
+        half_sev = keep.tile([P, N // P], F32, name="half_sev")
+        half_pi = keep.tile([P, 1], F32, name="half_pi")
+        warm = keep.tile([P, 1], F32, name="warm")
+        one = loads.tile([P, 14336], F32, name="one", offset=0)
+        tab_w = loads.tile([P, T], U32, name="tab_w", align_bytes=64, offset=0)
+        wr_first = loads.tile([P, 2 * BANK], U8, name="wr_first", align_bytes=64, offset=8192)
+        wr_rest = loads.tile([P, 2 * (H - BANK)], U8, name="wr_rest", align_bytes=64, offset=9216)
+        wf_w = loads.tile([P, BLOCKS, N], U32, name="wf_w", align_bytes=64, offset=12288)
         wgt_sb = loads.tile([P, M], F32, name="wgt_sb", offset=18432)
         phase_sb = loads.tile([P, BLOCKS, PACK], F32, name="phase_sb", offset=20480)
         bf_sb = loads.tile([P, N // P], F32, name="bf_sb", offset=20544)
         sev_sb = loads.tile([P, N // P], F32, name="sev_sb", offset=20608)
-        half_bf = keep.tile([P, N // P], F32, name="half_bf")
-        half_sev = keep.tile([P, N // P], F32, name="half_sev")
-        one = loads.tile([P, 3072], F32, name="one", offset=0)
-        pi = loads.tile([P, 11264], F32, name="pi", offset=12288)
-        half_pi = keep.tile([P, 1], F32, name="half_pi")
-        warm = keep.tile([P, 1], F32, name="warm")
+        tf_raw = loads.tile([P, PACK, M], F32, name="tf_raw", offset=24576)
+        wt_raw = [loads.tile([P, PACK, BANK], F32, name="wt_raw%d" % b, offset=32768 + 8192 * b) for b in range(BLOCKS)]
 
         nc.gpsimd.memset(tab_s[:].bitcast(I32), 0)
-        nc.vector.memset(one[:, 0:1], 1.0)
-        nc.vector.tensor_scalar(pi[:, 0:1], one[:, 0:1], math.pi, None, ALU.mult)
         nc.vector.memset(wr_s[:].bitcast(I32), 0)
-        nc.vector.tensor_scalar(half_pi[:], pi[:, 0:1], 0.5, None, ALU.mult)
+        nc.gpsimd.memset(one[:, 0:1], 1.0)
+        nc.vector.tensor_scalar(half_pi[:], one[:, 0:1], 0.5 * math.pi, None, ALU.mult)
         nc.scalar.activation(out=warm[:], in_=half_pi[:], func=ACT.Silu)
         nc.gpsimd.memset(wf_s[:].rearrange("p a c -> p (a c)").bitcast(I32), 0)
 
-        nc.sync.dma_start(idx[:], offs)
-        for q in range(4):
-            nc.sync.dma_start(tab_s[32 * q : 32 * q + 4, :].bitcast(I32), tab_scales[0, 4 * q : 4 * q + 4, :].bitcast(I32))
-        nc.sync.dma_start(tab_w[:].bitcast(I32), tab_words[0].rearrange("p t i -> p (t i)").bitcast(I32))
-        nc.sync.dma_start(wr_w[:].bitcast(I32), wr_words[0].bitcast(I32))
-        for q in range(4):
-            nc.sync.dma_start(wr_s[32 * q : 32 * q + 4, :].bitcast(I32), wr_scales[0, 4 * q : 4 * q + 4, :].bitcast(I32))
-        nc.sync.dma_start(idx2[:], offs2)
-        nc.sync.dma_start(wgt_sb[:], wgt)
+        def load_scale_rows(plane, rows):
+            for q in range(4):
+                nc.sync.dma_start(plane[32 * q : 32 * q + 4].bitcast(I32), rows[4 * q : 4 * q + 4].bitcast(I32))
 
-        tf_raw = loads.tile([P, PACK, M], F32, name="tf_raw", offset=24576)
+        def load_wt(b):
+            nc.sync.dma_start(wt_raw[b][:], wt[:, BANK * b : BANK * (b + 1)].rearrange("(p j) c -> p j c", j=PACK))
+
+        nc.sync.dma_start(idx[:], offs)
+        nc.sync.dma_start(idx2[:], offs2)
+        load_scale_rows(tab_s, tab_scales[0])
+        nc.sync.dma_start(wr_first[:].bitcast(I32), wr_words[0, :, 0 : 2 * BANK].bitcast(I32))
+        nc.sync.dma_start(tab_w[:].bitcast(I32), tab_words[0].rearrange("p t i -> p (t i)").bitcast(I32))
+        load_scale_rows(wr_s, wr_scales[0])
+        nc.sync.dma_start(wr_rest[:].bitcast(I32), wr_words[0, :, 2 * BANK :].bitcast(I32))
         nc.sync.dma_start(tf_raw[:], tf.rearrange("(p j) m -> p j m", j=PACK))
-        wt_raw = []
-        for b in range(BLOCKS):
-            raw = loads.tile([P, PACK, BANK], F32, name="wt_raw%d" % b, offset=32768 + 8192 * b)
-            nc.sync.dma_start(raw[:], wt[:, BANK * b : BANK * (b + 1)].rearrange("(p j) c -> p j c", j=PACK))
-            wt_raw.append(raw)
-            if b == 0:
-                nc.sync.dma_start(phase_sb[:], phase.rearrange("(b p i) -> p b i", b=BLOCKS, i=PACK))
-        nc.sync.dma_start(
-            wf_w[:].bitcast(I32), wf_words.rearrange("a p c i -> p a (c i)").bitcast(I32))
-        for q in range(4):
-            nc.sync.dma_start(
-                wf_s[32 * q : 32 * q + 4, :, :].bitcast(I32),
-                wf_scales[:, 4 * q : 4 * q + 4, :].rearrange("a r c -> r a c").bitcast(I32))
+        nc.sync.dma_start(wgt_sb[:], wgt)
+        load_wt(0)
+        nc.sync.dma_start(phase_sb[:], phase.rearrange("(b p i) -> p b i", b=BLOCKS, i=PACK))
+        load_wt(1)
+        load_wt(2)
+        nc.sync.dma_start(wf_w[:].bitcast(I32), wf_words.rearrange("a p c i -> p a (c i)").bitcast(I32))
+        load_scale_rows(wf_s, wf_scales.rearrange("a r c -> r a c"))
         with nc.allow_non_contiguous_dma(reason="one value a partition"):
             nc.sync.dma_start(bf_sb[:], bf.rearrange("(u p) -> p u", p=P))
             nc.sync.dma_start(sev_sb[:], sev.rearrange("(u p) -> p u", p=P))
 
-        def permute_wr(b):
+        def deal_words(b):
+            raw = wr_first[:] if b == 0 else wr_rest[:, 2 * BANK * (b - 1) : 2 * BANK * b]
             words = keep.tile([P, 2 * BANK], U8, name="wr_wp%d" % b, align_bytes=64)
-            scales = keep.tile([P, BANK], U8, name="wr_sp%d" % b, align_bytes=64)
             nc.vector.tensor_copy(
                 words[:].bitcast(U16).rearrange("p (t c e) -> p c t e", t=PACK, e=8),
-                wr_w[:, 2 * BANK * b : 2 * BANK * (b + 1)].bitcast(U16).rearrange("p (c e t) -> p c t e", t=PACK, e=8))
+                raw.bitcast(U16).rearrange("p (c e t) -> p c t e", t=PACK, e=8))
+            return words
+
+        def deal_scales(b):
+            scales = keep.tile([P, BANK], U8, name="wr_sp%d" % b, align_bytes=64)
             nc.vector.tensor_copy(
                 scales[:].rearrange("p (t c e) -> p c t e", t=PACK, e=16),
                 wr_s[:, BANK * b : BANK * (b + 1)].rearrange("p (c e t) -> p c t e", t=PACK, e=16))
-            return words, scales
+            return scales
 
-        def gather_table(window, dtype, name, half):
-            picked = keep.tile([P, BANK], dtype, name="%s%d" % (name, half), align_bytes=64)
-            nc.vector.tensor_copy(picked[:], window[:].indirect(idx[:, 32 * half : 32 * (half + 1)]))
+        def gather_words(half):
+            picked = loads.tile([P, BANK], U32, name="v_w%d" % half, align_bytes=64, offset=59392 - 2048 * half)
+            nc.vector.tensor_copy(picked[:], tab_w[:].indirect(idx[:, 32 * half : 32 * (half + 1)]))
             return picked
 
-        def quantise(grouped, name):
-            codes = keep.tile([P, BANK], U32, name=name + "_codes", align_bytes=64)
-            scales = keep.tile([P, BANK], U8, name=name + "_scales", align_bytes=64)
-            nc.vector.quantize_mx(out=codes[:].bitcast(FP8X4), scales=scales[:], in_=grouped[:])
+        def quantise(grouped, width, name):
+            codes = keep.tile([P, width], U32, name=name + "_codes", align_bytes=64)
+            scales = keep.tile([P, width], U8, name=name + "_scales", align_bytes=64)
+            nc.vector.quantize_mx(out=codes[:].bitcast(FP8X4), scales=scales[:], in_=grouped)
             return codes, scales
 
-        def group_wt(b, on_scalar):
-            grouped = ring.tile([P, PACK * BANK], BF16, name="wt_grouped", align_bytes=64)
-            dst = grouped[:].rearrange("p (t c j) -> p c t j", t=PACK, j=PACK)
-            src = wt_raw[b][:].rearrange("p j (c t) -> p c t j", t=PACK)
-            if on_scalar:
-                nc.scalar.copy(dst, src)
-            else:
-                nc.vector.tensor_copy(dst, src)
-            return grouped
+        def group_wt(b, grouped, copy, lo=0, hi=P):
+            copy(grouped.rearrange("p (t c j) -> p c t j", t=PACK, j=PACK)[:, lo:hi],
+                 wt_raw[b][:].rearrange("p j (c t) -> p c t j", t=PACK)[:, lo:hi])
 
-        def project(b, wr_p, v):
+        def project(b, order):
             planes = [keep.tile([P, S], F32, name="h%d_%d" % (b, t)) for t in range(PACK)]
-            for t in range(PACK):
-                for half in range(2):
-                    acc = psum.tile([P, BANK], F32, name="acc")
-                    nc.tensor.matmul_mx(
-                        out=acc[:], lhsT=wr_p[0][:, 2 * P * t : 2 * P * (t + 1)].bitcast(FP4X4),
-                        lhsT_scale=wr_p[1][:, P * t : P * (t + 1)],
-                        rhs=v[half][0][:].bitcast(FP8X4), rhs_scale=v[half][1][:], start=True, stop=True)
-                    nc.scalar.copy(planes[t][:, BANK * half : BANK * (half + 1)], acc[:])
+            for t, half in order:
+                acc = psum.tile([P, BANK], F32, name="h_acc", tag="y" if b == BLOCKS - 1 and t >= 2 else "acc")
+                nc.tensor.matmul_mx(
+                    out=acc[:], lhsT=wr_w[b][:, 2 * P * t : 2 * P * (t + 1)].bitcast(FP4X4),
+                    lhsT_scale=wr_p[b][:, P * t : P * (t + 1)],
+                    rhs=v_w[half][:].bitcast(FP8X4), rhs_scale=v_s[:, BANK * half : BANK * (half + 1)],
+                    start=True, stop=True)
+                nc.scalar.copy(planes[t][:, BANK * half : BANK * (half + 1)], acc[:])
             return planes
 
-        def magnitudes(b, wt_q, tf_q):
-            size = ring.tile([P, PACK, M], F32, name="size")
+        def magnitudes(b):
+            codes, scales, first = wt_q[b]
             for t in range(PACK):
-                acc = psum.tile([P, BANK], F32, name="acc")
+                cols = slice(first + P * t, first + P * (t + 1))
+                acc = psum.tile([P, BANK], F32, name="angle", tag="y" if b == 1 else "acc")
                 nc.tensor.matmul_mx(
-                    out=acc[:], lhsT=wt_q[0][:, P * t : P * (t + 1)].bitcast(FP8X4),
-                    lhsT_scale=wt_q[1][:, P * t : P * (t + 1)],
-                    rhs=tf_q[0][:].bitcast(FP8X4), rhs_scale=tf_q[1][:], start=True, stop=True)
-                nc.scalar.activation(out=size[:, t, :], in_=acc[:], func=ACT.Abs, bias=phase_sb[:, b, t : t + 1])
-            return size
+                    out=acc[:], lhsT=codes[:, cols].bitcast(FP8X4), lhsT_scale=scales[:, cols],
+                    rhs=early_q[0][:, 0:M].bitcast(FP8X4), rhs_scale=early_q[1][:, 0:M], start=True, stop=True)
+                nc.scalar.activation(out=size(b, 1)[:, t, :], in_=acc[:], func=ACT.Abs, bias=phase_sb[:, b, t : t + 1])
 
         def pick(b, planes):
-            x = keep.tile([P, PACK, M], F32, name="x%d" % b)
+            x = loads.tile([P, PACK, M], F32, name="x%d" % b, offset=61440 + 8192 * (BLOCKS - 1 - b))
             for t in range(PACK):
                 nc.vector.tensor_tensor(x[:, t, :], planes[t][:].indirect(idx2[:]), wgt_sb[:], ALU.mult)
             return x
 
-        def cosine(size, lo, width):
-            cos = ring.tile([P, PACK, width], F32, name="cos%d" % width, bufs=2 if width == M else 4)
-            nc.scalar.activation(out=cos[:], in_=size[:, :, lo : lo + width], func=ACT.Sin, bias=half_pi[:], scale=-1.0)
+        def cosine(first, count, lo, width):
+            cos = keep.tile([P, PACK * count, width], F32, name="cos%d_%d" % (first, lo))
+            nc.scalar.activation(out=cos[:], in_=size(first, count)[:, :, lo : lo + width],
+                                 func=ACT.Sin, bias=half_pi[:], scale=-1.0)
             return cos
 
-        def modulate(b, x, cos, lo, width):
-            z = ring.tile([P, PACK * width], BF16, name="z%d" % width, align_bytes=64, bufs=2 if width == M else 4)
+        def modulate(b, cos, lo, width):
+            z = keep.tile([P, PACK * width], BF16, name="z%d_%d" % (b, lo), align_bytes=64)
             nc.vector.tensor_tensor(
                 z[:].rearrange("p (c e t) -> p c t e", t=PACK, e=2),
-                x[:, :, lo : lo + width].rearrange("p t (c e) -> p c t e", e=2),
+                x[b][:, :, lo : lo + width].rearrange("p t (c e) -> p c t e", e=2),
                 cos.rearrange("p t (c e) -> p c t e", e=2), ALU.mult)
-            codes = keep.tile([P, width], U32, name="z_codes%d_%d" % (b, lo), align_bytes=64)
-            scales = keep.tile([P, width], U8, name="z_scales%d_%d" % (b, lo), align_bytes=64)
-            nc.vector.quantize_mx(out=codes[:].bitcast(FP8X4), scales=scales[:], in_=z[:])
-            return codes, scales
+            return z
 
-        def forecast_pass(acc, u, b, codes, scales):
-            nc.tensor.matmul_mx(
-                out=acc, lhsT=wf_w[:, b, P * u : P * (u + 1)].bitcast(FP8X4),
-                lhsT_scale=wf_s[:, b, P * u : P * (u + 1)],
-                rhs=codes.bitcast(FP8X4), rhs_scale=scales, start=(b == 0), stop=(b == BLOCKS - 1))
+        v_s = keep.tile([P, S], U8, name="v_s", align_bytes=64)
+        nc.vector.tensor_copy(v_s[:], tab_s[:].indirect(idx[:]))
+        wr_w = [deal_words(0)]
+        v_w = [gather_words(0)]
+        wr_p = [deal_scales(b) for b in range(BLOCKS)]
+        v_w.append(gather_words(1))
+        wr_w.extend(deal_words(b) for b in range(1, BLOCKS))
 
-        v_s = [gather_table(tab_s, U8, "v_s", half) for half in range(2)]
-        wr_p = [permute_wr(0)]
-        v = [(gather_table(tab_w, U32, "v_w", half), v_s[half]) for half in range(2)]
-        wr_p.extend(permute_wr(b) for b in range(1, BLOCKS))
-        planes = [project(b, wr_p[b], v) for b in range(BLOCKS)]
+        by_half = [(t, half) for half in range(2) for t in range(PACK)]
+        by_plane = [(t, half) for t in range(PACK) for half in range(2)]
+        early = keep.tile([P, 2, PACK * BANK], BF16, name="early", align_bytes=64)
+        late = loads.tile([P, 2, PACK * BANK], BF16, name="late", align_bytes=64, offset=61440)
+        planes = [project(0, by_half), project(1, by_plane)]
+        group_wt(1, late[:, 0, :], nc.scalar.copy)
+        planes.append(project(2, by_plane))
 
-        tf_grouped = ring.tile([P, PACK * M], BF16, name="wt_grouped", align_bytes=64)
         nc.vector.tensor_copy(
-            tf_grouped[:].rearrange("p (c e j) -> p c j e", j=PACK, e=4),
+            early[:, 0, :].rearrange("p (c e j) -> p c j e", j=PACK, e=4),
             tf_raw[:].rearrange("p j (c e) -> p c j e", e=4))
-        last = BLOCKS - 1
-        tf_q = quantise(tf_grouped, "tf")
-        wt_q = [quantise(group_wt(b, b == last), "wt%d" % b) for b in range(BLOCKS)]
-        x = [pick(b, planes[b]) for b in range(BLOCKS)]
+        group_wt(0, early[:, 1, :], nc.vector.tensor_copy)
+        x = [pick(0, planes[0])]
+        early_q = quantise(early[:].rearrange("p a c -> p (a c)"), 2 * BANK, "early")
+        group_wt(2, late[:, 1, :], nc.vector.tensor_copy)
+        x.append(pick(1, planes[1]))
+        late_q = quantise(late[:].rearrange("p a c -> p (a c)"), 2 * BANK, "late")
+        x.append(pick(2, planes[2]))
+        wt_q = [early_q + (BANK,), late_q + (0,), late_q + (BANK,)]
         nc.scalar.mul(half_bf[:], bf_sb[:], 0.5)
         nc.scalar.mul(half_sev[:], sev_sb[:], 0.5)
 
-        z_q = [modulate(b, x[b], cosine(magnitudes(b, wt_q[b], tf_q), 0, M)[:], 0, M) for b in range(last)]
-        size = magnitudes(last, wt_q[last], tf_q)
-        z_last = [modulate(last, x[last], cosine(size, lo, QUARTER)[:], lo, QUARTER) for lo in range(0, M, QUARTER)]
+        size_first = loads.tile([P, PACK, M], F32, name="size_first", offset=0)
+        size_rest = loads.tile([P, (BLOCKS - 1) * PACK, M], F32, name="size_rest", offset=24576)
+
+        def size(first, count):
+            if first == 0:
+                return size_first[:]
+            return size_rest[:, PACK * (first - 1) : PACK * (first - 1 + count), :]
+
+        magnitudes(0)
+        z_first = quantise(modulate(0, cosine(0, 1, 0, M)[:], 0, M)[:], M, "z0")
+        lead = []
+        for b in range(1, BLOCKS):
+            magnitudes(b)
+            lead.append(cosine(b, 1, *PIECES[0])[:])
 
         types = N // P
         out_v = out.rearrange("(u p) m -> p u m", p=P)
-        for piece in range(M // QUARTER):
-            cols = slice(QUARTER * piece, QUARTER * (piece + 1))
-            accs = [psum.tile([P, QUARTER], F32, name="y%d_%d" % (piece, u), tag="acc" if piece % 2 else "y") for u in range(types)]
-            for u in range(types):
-                for b in range(last):
-                    forecast_pass(accs[u][:], u, b, z_q[b][0][:, cols], z_q[b][1][:, cols])
-            for u in range(types):
-                forecast_pass(accs[u][:], u, last, z_last[piece][0][:], z_last[piece][1][:])
-            group = 2 if piece == M // QUARTER - 1 else types
+
+        rest = [lead]
+        for lo, width in PIECES[1:]:
+            both = cosine(1, BLOCKS - 1, lo, width)
+            rest.append([both[:, PACK * i : PACK * (i + 1), :] for i in range(BLOCKS - 1)])
+
+        def prepare(piece):
+            lo, width = PIECES[piece]
+            cos = rest[piece]
+            z = [modulate(b, cos[b - 1], lo, width) for b in range(1, BLOCKS)]
+            return [quantise(z[b - 1][:], width, "z%d_%d" % (b, lo)) for b in range(1, BLOCKS)]
+
+        def forecast(piece, z_q):
+            lo, width = PIECES[piece]
+            cols = slice(lo, lo + width)
+            operands = [(z_first[0][:, cols], z_first[1][:, cols])] + [(c[:], s[:]) for c, s in z_q]
+            accs = [psum.tile([P, width], F32, name="y%d_%d" % (piece, u), tag="y" if piece % 2 else "acc") for u in range(types)]
+            for b in range(BLOCKS):
+                for u in range(types):
+                    nc.tensor.matmul_mx(
+                        out=accs[u][:], lhsT=wf_w[:, b, P * u : P * (u + 1)].bitcast(FP8X4),
+                        lhsT_scale=wf_s[:, b, P * u : P * (u + 1)],
+                        rhs=operands[b][0].bitcast(FP8X4), rhs_scale=operands[b][1],
+                        start=(b == 0), stop=(b == BLOCKS - 1))
+            group = 2 if piece == len(PIECES) - 1 else types
             for first in range(0, types, group):
-                res = ring.tile([P, group, QUARTER], F32, name="res", bufs=5)
+                res = keep.tile([P, group, width], F32, name="res%d_%d" % (piece, first))
                 for u in range(first, first + group):
-                    tanh = ring.tile([P, QUARTER], F32, name="tanh", bufs=16)
+                    tanh = loads.tile([P, width], F32, name="tanh%d_%d" % (piece, u), offset=24576 + 4 * (M * u + lo))
                     nc.scalar.activation(out=tanh[:], in_=accs[u][:], func=ACT.Tanh, bias=half_bf[:, u : u + 1], scale=0.5)
                     nc.vector.tensor_scalar(res[:, u - first, :], tanh[:], half_sev[:, u : u + 1], half_sev[:, u : u + 1], ALU.mult, ALU.add)
                 nc.sync.dma_start(out_v[:, first : first + group, cols], res[:])
+
+        ahead = prepare(0)
+        for piece in range(len(PIECES)):
+            z_q = ahead
+            if piece + 1 < len(PIECES):
+                ahead = prepare(piece + 1)
+            forecast(piece, z_q)

@@ -23,6 +23,7 @@ BLOCKS = H // (P * PACK)
 BANK = 512
 HALF = M // 2
 QUARTER = M // 4
+SHARE = 64
 PIECES = [(0, HALF), (HALF, QUARTER), (HALF + QUARTER, QUARTER)]
 
 
@@ -78,9 +79,9 @@ def tile_list_event_graph_forecast_kernel(
         nc.sync.dma_start(tab_w[:].bitcast(I32), tab_words[0].rearrange("p t i -> p (t i)").bitcast(I32))
         load_scale_rows(wr_s, wr_scales[0])
         nc.sync.dma_start(wr_rest[:].bitcast(I32), wr_words[0, :, 2 * BANK :].bitcast(I32))
-        nc.sync.dma_start(tf_raw[:], tf.rearrange("(p j) m -> p j m", j=PACK))
-        nc.sync.dma_start(wgt_sb[:], wgt)
         load_wt(0)
+        nc.sync.dma_start(wgt_sb[:], wgt)
+        nc.sync.dma_start(tf_raw[:], tf.rearrange("(p j) m -> p j m", j=PACK))
         nc.sync.dma_start(phase_sb[:], phase.rearrange("(b p i) -> p b i", b=BLOCKS, i=PACK))
         load_wt(1)
         load_wt(2)
@@ -139,7 +140,7 @@ def tile_list_event_graph_forecast_kernel(
                 acc = psum.tile([P, BANK], F32, name="angle", tag="y" if b == 1 else "acc")
                 nc.tensor.matmul_mx(
                     out=acc[:], lhsT=codes[:, cols].bitcast(FP8X4), lhsT_scale=scales[:, cols],
-                    rhs=early_q[0][:, 0:M].bitcast(FP8X4), rhs_scale=early_q[1][:, 0:M], start=True, stop=True)
+                    rhs=tf_q[0][:].bitcast(FP8X4), rhs_scale=tf_q[1][:], start=True, stop=True)
                 nc.scalar.activation(out=size(b, 1)[:, t, :], in_=acc[:], func=ACT.Abs, bias=phase_sb[:, b, t : t + 1])
 
         def pick(b, planes):
@@ -172,23 +173,27 @@ def tile_list_event_graph_forecast_kernel(
 
         by_half = [(t, half) for half in range(2) for t in range(PACK)]
         by_plane = [(t, half) for t in range(PACK) for half in range(2)]
-        early = keep.tile([P, 2, PACK * BANK], BF16, name="early", align_bytes=64)
-        late = loads.tile([P, 2, PACK * BANK], BF16, name="late", align_bytes=64, offset=61440)
-        planes = [project(0, by_half), project(1, by_plane)]
-        group_wt(1, late[:, 0, :], nc.scalar.copy)
+        early = loads.tile([P, 2, PACK * BANK], BF16, name="early", align_bytes=64, offset=61440)
+        late = keep.tile([P, PACK * BANK], BF16, name="late", align_bytes=64)
+        tf_grouped = loads.tile([P, PACK * M], BF16, name="tf_grouped", align_bytes=64, offset=69632)
+        planes = [project(0, by_half)]
+        nc.scalar.copy(
+            tf_grouped[:].rearrange("p (c e j) -> p c j e", j=PACK, e=4),
+            tf_raw[:].rearrange("p j (c e) -> p c j e", e=4))
+        planes.append(project(1, by_plane))
+        group_wt(1, early[:, 0, :], nc.scalar.copy, 0, SHARE)
         planes.append(project(2, by_plane))
 
-        nc.vector.tensor_copy(
-            early[:, 0, :].rearrange("p (c e j) -> p c j e", j=PACK, e=4),
-            tf_raw[:].rearrange("p j (c e) -> p c j e", e=4))
-        group_wt(0, early[:, 1, :], nc.vector.tensor_copy)
+        group_wt(0, late[:], nc.vector.tensor_copy)
         x = [pick(0, planes[0])]
-        early_q = quantise(early[:].rearrange("p a c -> p (a c)"), 2 * BANK, "early")
-        group_wt(2, late[:, 1, :], nc.vector.tensor_copy)
+        late_q = quantise(late[:], BANK, "late")
+        group_wt(1, early[:, 0, :], nc.vector.tensor_copy, SHARE, P)
+        tf_q = quantise(tf_grouped[:], M, "tf")
         x.append(pick(1, planes[1]))
-        late_q = quantise(late[:].rearrange("p a c -> p (a c)"), 2 * BANK, "late")
+        group_wt(2, early[:, 1, :], nc.vector.tensor_copy)
+        early_q = quantise(early[:].rearrange("p a c -> p (a c)"), 2 * BANK, "early")
         x.append(pick(2, planes[2]))
-        wt_q = [early_q + (BANK,), late_q + (0,), late_q + (BANK,)]
+        wt_q = [late_q + (0,), early_q + (0,), early_q + (BANK,)]
         nc.scalar.mul(half_bf[:], bf_sb[:], 0.5)
         nc.scalar.mul(half_sev[:], sev_sb[:], 0.5)
 
@@ -233,7 +238,7 @@ def tile_list_event_graph_forecast_kernel(
                         lhsT_scale=wf_s[:, b, P * u : P * (u + 1)],
                         rhs=operands[b][0].bitcast(FP8X4), rhs_scale=operands[b][1],
                         start=(b == 0), stop=(b == BLOCKS - 1))
-            group = 2 if piece == len(PIECES) - 1 else types
+            group = 1 if piece == len(PIECES) - 1 else types
             for first in range(0, types, group):
                 res = keep.tile([P, group, width], F32, name="res%d_%d" % (piece, first))
                 for u in range(first, first + group):

@@ -48,8 +48,8 @@ def tile_list_event_graph_forecast_kernel(
         warm = keep.tile([P, 1], F32, name="warm")
         one = loads.tile([P, 14336], F32, name="one", offset=0)
         tab_w = loads.tile([P, T], U32, name="tab_w", align_bytes=64, offset=0)
-        wr_first = loads.tile([P, 2 * BANK], U8, name="wr_first", align_bytes=64, offset=8192)
-        wr_rest = loads.tile([P, 2 * (H - BANK)], U8, name="wr_rest", align_bytes=64, offset=9216)
+        wr_first = keep.tile([P, 4 * BANK], U8, name="wr_first", align_bytes=64)
+        wr_rest = loads.tile([P, 2 * BANK], U8, name="wr_rest", align_bytes=64, offset=9216)
         wf_w = loads.tile([P, BLOCKS, N], U32, name="wf_w", align_bytes=64, offset=12288)
         wgt_sb = loads.tile([P, M], F32, name="wgt_sb", offset=18432)
         phase_sb = loads.tile([P, BLOCKS, PACK], F32, name="phase_sb", offset=20480)
@@ -72,13 +72,13 @@ def tile_list_event_graph_forecast_kernel(
         def load_wt(b):
             nc.sync.dma_start(wt_raw[b][:], wt[:, BANK * b : BANK * (b + 1)].rearrange("(p j) c -> p j c", j=PACK))
 
+        nc.sync.dma_start(wr_first[:].bitcast(I32), wr_words[0, :, 0 : 4 * BANK].bitcast(I32))
         nc.sync.dma_start(idx[:], offs)
         nc.sync.dma_start(idx2[:], offs2)
         load_scale_rows(tab_s, tab_scales[0])
-        nc.sync.dma_start(wr_first[:].bitcast(I32), wr_words[0, :, 0 : 2 * BANK].bitcast(I32))
         nc.sync.dma_start(tab_w[:].bitcast(I32), tab_words[0].rearrange("p t i -> p (t i)").bitcast(I32))
         load_scale_rows(wr_s, wr_scales[0])
-        nc.sync.dma_start(wr_rest[:].bitcast(I32), wr_words[0, :, 2 * BANK :].bitcast(I32))
+        nc.sync.dma_start(wr_rest[:].bitcast(I32), wr_words[0, :, 4 * BANK :].bitcast(I32))
         load_wt(0)
         nc.sync.dma_start(wgt_sb[:], wgt)
         nc.sync.dma_start(tf_raw[:], tf.rearrange("(p j) m -> p j m", j=PACK))
@@ -92,7 +92,7 @@ def tile_list_event_graph_forecast_kernel(
             nc.sync.dma_start(sev_sb[:], sev.rearrange("(u p) -> p u", p=P))
 
         def deal_words(b):
-            raw = wr_first[:] if b == 0 else wr_rest[:, 2 * BANK * (b - 1) : 2 * BANK * b]
+            raw = wr_rest[:] if b == BLOCKS - 1 else wr_first[:, 2 * BANK * b : 2 * BANK * (b + 1)]
             words = keep.tile([P, 2 * BANK], U8, name="wr_wp%d" % b, align_bytes=64)
             nc.vector.tensor_copy(
                 words[:].bitcast(U16).rearrange("p (t c e) -> p c t e", t=PACK, e=8),
@@ -123,8 +123,8 @@ def tile_list_event_graph_forecast_kernel(
 
         def project(b, order):
             planes = [keep.tile([P, S], F32, name="h%d_%d" % (b, t)) for t in range(PACK)]
-            for t, half in order:
-                acc = psum.tile([P, BANK], F32, name="h_acc", tag="y" if b == BLOCKS - 1 and t >= 2 else "acc")
+            for step, (t, half) in enumerate(order):
+                acc = psum.tile([P, BANK], F32, name="h_acc", tag="acc" if step < PACK else "y")
                 nc.tensor.matmul_mx(
                     out=acc[:], lhsT=wr_w[b][:, 2 * P * t : 2 * P * (t + 1)].bitcast(FP4X4),
                     lhsT_scale=wr_p[b][:, P * t : P * (t + 1)],
@@ -140,11 +140,11 @@ def tile_list_event_graph_forecast_kernel(
                 acc = psum.tile([P, BANK], F32, name="angle", tag="y" if b == 1 else "acc")
                 nc.tensor.matmul_mx(
                     out=acc[:], lhsT=codes[:, cols].bitcast(FP8X4), lhsT_scale=scales[:, cols],
-                    rhs=tf_q[0][:].bitcast(FP8X4), rhs_scale=tf_q[1][:], start=True, stop=True)
+                    rhs=early_q[0][:, 0:M].bitcast(FP8X4), rhs_scale=early_q[1][:, 0:M], start=True, stop=True)
                 nc.scalar.activation(out=size(b, 1)[:, t, :], in_=acc[:], func=ACT.Abs, bias=phase_sb[:, b, t : t + 1])
 
         def pick(b, planes):
-            x = loads.tile([P, PACK, M], F32, name="x%d" % b, offset=61440 + 8192 * (BLOCKS - 1 - b))
+            x = keep.tile([P, PACK, M], F32, name="x%d" % b)
             for t in range(PACK):
                 nc.vector.tensor_tensor(x[:, t, :], planes[t][:].indirect(idx2[:]), wgt_sb[:], ALU.mult)
             return x
@@ -163,37 +163,35 @@ def tile_list_event_graph_forecast_kernel(
                 cos.rearrange("p t (c e) -> p c t e", e=2), ALU.mult)
             return z
 
+        wr_w = [deal_words(b) for b in range(BLOCKS - 1)]
         v_s = keep.tile([P, S], U8, name="v_s", align_bytes=64)
         nc.vector.tensor_copy(v_s[:], tab_s[:].indirect(idx[:]))
-        wr_w = [deal_words(0)]
         v_w = [gather_words(0)]
         wr_p = [deal_scales(b) for b in range(BLOCKS)]
         v_w.append(gather_words(1))
-        wr_w.extend(deal_words(b) for b in range(1, BLOCKS))
+        wr_w.append(deal_words(BLOCKS - 1))
 
         by_half = [(t, half) for half in range(2) for t in range(PACK)]
         by_plane = [(t, half) for t in range(PACK) for half in range(2)]
-        early = loads.tile([P, 2, PACK * BANK], BF16, name="early", align_bytes=64, offset=61440)
-        late = keep.tile([P, PACK * BANK], BF16, name="late", align_bytes=64)
-        tf_grouped = loads.tile([P, PACK * M], BF16, name="tf_grouped", align_bytes=64, offset=69632)
+        early = keep.tile([P, 2, PACK * BANK], BF16, name="early", align_bytes=64)
+        late = keep.tile([P, 2, PACK * BANK], BF16, name="late", align_bytes=64)
         planes = [project(0, by_half)]
         nc.scalar.copy(
-            tf_grouped[:].rearrange("p (c e j) -> p c j e", j=PACK, e=4),
+            early[:, 0, :].rearrange("p (c e j) -> p c j e", j=PACK, e=4),
             tf_raw[:].rearrange("p j (c e) -> p c j e", e=4))
         planes.append(project(1, by_plane))
-        group_wt(1, early[:, 0, :], nc.scalar.copy, 0, SHARE)
+        group_wt(1, late[:, 0, :], nc.scalar.copy, 0, SHARE)
         planes.append(project(2, by_plane))
 
-        group_wt(0, late[:], nc.vector.tensor_copy)
+        group_wt(0, early[:, 1, :], nc.vector.tensor_copy)
         x = [pick(0, planes[0])]
-        late_q = quantise(late[:], BANK, "late")
-        group_wt(1, early[:, 0, :], nc.vector.tensor_copy, SHARE, P)
-        tf_q = quantise(tf_grouped[:], M, "tf")
-        x.append(pick(1, planes[1]))
-        group_wt(2, early[:, 1, :], nc.vector.tensor_copy)
         early_q = quantise(early[:].rearrange("p a c -> p (a c)"), 2 * BANK, "early")
+        group_wt(1, late[:, 0, :], nc.vector.tensor_copy, SHARE, P)
+        group_wt(2, late[:, 1, :], nc.vector.tensor_copy)
+        x.append(pick(1, planes[1]))
+        late_q = quantise(late[:].rearrange("p a c -> p (a c)"), 2 * BANK, "late")
         x.append(pick(2, planes[2]))
-        wt_q = [late_q + (0,), early_q + (0,), early_q + (BANK,)]
+        wt_q = [early_q + (BANK,), late_q + (0,), late_q + (BANK,)]
         nc.scalar.mul(half_bf[:], bf_sb[:], 0.5)
         nc.scalar.mul(half_sev[:], sev_sb[:], 0.5)
 
@@ -206,7 +204,9 @@ def tile_list_event_graph_forecast_kernel(
             return size_rest[:, PACK * (first - 1) : PACK * (first - 1 + count), :]
 
         magnitudes(0)
-        z_first = quantise(modulate(0, cosine(0, 1, 0, M)[:], 0, M)[:], M, "z0")
+        cos_first = cosine(0, 1, 0, M)
+        z_halves = [modulate(0, cos_first[:, :, lo : lo + HALF], lo, HALF) for lo in (0, HALF)]
+        z_first = [quantise(z_halves[i][:], HALF, "z0_%d" % i) for i in range(2)]
         lead = []
         for b in range(1, BLOCKS):
             magnitudes(b)
@@ -229,7 +229,8 @@ def tile_list_event_graph_forecast_kernel(
         def forecast(piece, z_q):
             lo, width = PIECES[piece]
             cols = slice(lo, lo + width)
-            operands = [(z_first[0][:, cols], z_first[1][:, cols])] + [(c[:], s[:]) for c, s in z_q]
+            within = slice(lo % HALF, lo % HALF + width)
+            operands = [(z_first[lo // HALF][0][:, within], z_first[lo // HALF][1][:, within])] + [(c[:], s[:]) for c, s in z_q]
             accs = [psum.tile([P, width], F32, name="y%d_%d" % (piece, u), tag="y" if piece % 2 else "acc") for u in range(types)]
             for b in range(BLOCKS):
                 for u in range(types):

@@ -118,8 +118,8 @@ def tile_list_event_graph_forecast_kernel(
             return codes, scales
 
         def group_wt(b, grouped, copy, lo=0, hi=P):
-            copy(grouped.rearrange("p (t c j) -> p c t j", t=PACK, j=PACK)[:, lo:hi],
-                 wt_raw[b][:].rearrange("p j (c t) -> p c t j", t=PACK)[:, lo:hi])
+            copy(grouped.rearrange("p (t c j) -> p c j t", t=PACK, j=PACK)[:, lo:hi],
+                 wt_raw[b][:].rearrange("p j (c t) -> p c j t", t=PACK)[:, lo:hi])
 
         def project(b, order):
             planes = [keep.tile([P, S], F32, name="h%d_%d" % (b, t)) for t in range(PACK)]

@@ -95,15 +95,15 @@ def tile_list_event_graph_forecast_kernel(
             raw = wr_rest[:] if b == BLOCKS - 1 else wr_first[:, 2 * BANK * b : 2 * BANK * (b + 1)]
             words = keep.tile([P, 2 * BANK], U8, name="wr_wp%d" % b, align_bytes=64)
             nc.vector.tensor_copy(
-                words[:].bitcast(U16).rearrange("p (t c e) -> p c t e", t=PACK, e=8),
-                raw.bitcast(U16).rearrange("p (c e t) -> p c t e", t=PACK, e=8))
+                words[:].bitcast(U16).rearrange("p (t c) -> p c t", t=PACK),
+                raw.bitcast(U16).rearrange("p (c t) -> p c t", t=PACK))
             return words
 
         def deal_scales(b):
             scales = keep.tile([P, BANK], U8, name="wr_sp%d" % b, align_bytes=64)
             nc.vector.tensor_copy(
-                scales[:].rearrange("p (t c e) -> p c t e", t=PACK, e=16),
-                wr_s[:, BANK * b : BANK * (b + 1)].rearrange("p (c e t) -> p c t e", t=PACK, e=16))
+                scales[:].rearrange("p (t c) -> p c t", t=PACK),
+                wr_s[:, BANK * b : BANK * (b + 1)].rearrange("p (c t) -> p c t", t=PACK))
             return scales
 
         def gather_words(half):

@@ -35,18 +35,18 @@ def tile_list_event_graph_forecast_kernel(
     with ExitStack() as ctx:
         keep = ctx.enter_context(tc.tile_pool(name="keep", bufs=1))
         loads = ctx.enter_context(tc.tile_pool(name="loads", bufs=1))
-        psum = ctx.enter_context(tc.psum_pool(name="psum", bufs=4))
+        psum = ctx.enter_context(tc.psum_pool(name="psum", bufs=1))
 
         idx = keep.tile([P, S // 16], U16, name="idx")
         idx2 = keep.tile([P, M // 16], U16, name="idx2")
         tab_s = keep.tile([P, T], U8, name="tab_s", align_bytes=64)
-        wr_s = loads.tile([P, H], U8, name="wr_s", align_bytes=64, offset=57344)
+        wr_s = loads.tile([P, H], U8, name="wr_s", align_bytes=64, offset=73728)
         wf_s = keep.tile([P, BLOCKS, N], U8, name="wf_s", align_bytes=64)
         half_bf = keep.tile([P, N // P], F32, name="half_bf")
         half_sev = keep.tile([P, N // P], F32, name="half_sev")
         half_pi = keep.tile([P, 1], F32, name="half_pi")
         warm = keep.tile([P, 1], F32, name="warm")
-        one = loads.tile([P, 14336], F32, name="one", offset=0)
+        one = loads.tile([P, 18432], F32, name="one", offset=0)
         tab_w = loads.tile([P, T], U32, name="tab_w", align_bytes=64, offset=0)
         wr_first = keep.tile([P, 4 * BANK], U8, name="wr_first", align_bytes=64)
         wr_rest = loads.tile([P, 2 * BANK], U8, name="wr_rest", align_bytes=64, offset=9216)
@@ -55,7 +55,8 @@ def tile_list_event_graph_forecast_kernel(
         phase_sb = loads.tile([P, BLOCKS, PACK], F32, name="phase_sb", offset=20480)
         bf_sb = loads.tile([P, N // P], F32, name="bf_sb", offset=20544)
         sev_sb = loads.tile([P, N // P], F32, name="sev_sb", offset=20608)
-        tf_raw = loads.tile([P, PACK, M], F32, name="tf_raw", offset=24576)
+        tf_raw = [loads.tile([P, PACK, S], F32, name="tf_raw0", offset=57344)[:, :, 0:HALF],
+                  loads.tile([P, PACK, HALF], F32, name="tf_raw1", offset=24576)[:]]
         wt_raw = [loads.tile([P, PACK, BANK], F32, name="wt_raw%d" % b, offset=32768 + 8192 * b) for b in range(BLOCKS)]
 
         nc.gpsimd.memset(tab_s[:].bitcast(I32), 0)
@@ -72,16 +73,25 @@ def tile_list_event_graph_forecast_kernel(
         def load_wt(b):
             nc.sync.dma_start(wt_raw[b][:], wt[:, BANK * b : BANK * (b + 1)].rearrange("(p j) c -> p j c", j=PACK))
 
+        def load_tf(i):
+            nc.sync.dma_start(tf_raw[i], tf[:, HALF * i : HALF * (i + 1)].rearrange("(p j) m -> p j m", j=PACK))
+
+        def group_tf(i):
+            nc.scalar.copy(
+                early[:, 0, PACK * HALF * i : PACK * HALF * (i + 1)].rearrange("p (c e j) -> p c j e", j=PACK, e=4),
+                tf_raw[i].rearrange("p j (c e) -> p c j e", e=4))
+
         nc.sync.dma_start(wr_first[:].bitcast(I32), wr_words[0, :, 0 : 4 * BANK].bitcast(I32))
         nc.sync.dma_start(idx[:], offs)
         nc.sync.dma_start(idx2[:], offs2)
         load_scale_rows(tab_s, tab_scales[0])
         nc.sync.dma_start(tab_w[:].bitcast(I32), tab_words[0].rearrange("p t i -> p (t i)").bitcast(I32))
         load_scale_rows(wr_s, wr_scales[0])
+        load_tf(0)
         nc.sync.dma_start(wr_rest[:].bitcast(I32), wr_words[0, :, 4 * BANK :].bitcast(I32))
         load_wt(0)
         nc.sync.dma_start(wgt_sb[:], wgt)
-        nc.sync.dma_start(tf_raw[:], tf.rearrange("(p j) m -> p j m", j=PACK))
+        load_tf(1)
         nc.sync.dma_start(phase_sb[:], phase.rearrange("(b p i) -> p b i", b=BLOCKS, i=PACK))
         load_wt(1)
         load_wt(2)
@@ -107,12 +117,15 @@ def tile_list_event_graph_forecast_kernel(
             return scales
 
         def gather_words(half):
-            picked = loads.tile([P, BANK], U32, name="v_w%d" % half, align_bytes=64, offset=59392 - 2048 * half)
+            picked = loads.tile([P, BANK], U32, name="v_w%d" % half, align_bytes=64, offset=75776 - 2048 * half)
             nc.vector.tensor_copy(picked[:], tab_w[:].indirect(idx[:, 32 * half : 32 * (half + 1)]))
             return picked
 
-        def quantise(grouped, width, name):
-            codes = keep.tile([P, width], U32, name=name + "_codes", align_bytes=64)
+        def quantise(grouped, width, name, offset=None):
+            if offset is None:
+                codes = keep.tile([P, width], U32, name=name + "_codes", align_bytes=64)
+            else:
+                codes = loads.tile([P, width], U32, name=name + "_codes", align_bytes=64, offset=offset)
             scales = keep.tile([P, width], U8, name=name + "_scales", align_bytes=64)
             nc.vector.quantize_mx(out=codes[:].bitcast(FP8X4), scales=scales[:], in_=grouped)
             return codes, scales
@@ -122,9 +135,10 @@ def tile_list_event_graph_forecast_kernel(
                  wt_raw[b][:].rearrange("p j (c t) -> p c j t", t=PACK)[:, lo:hi])
 
         def project(b, order):
-            planes = [keep.tile([P, S], F32, name="h%d_%d" % (b, t)) for t in range(PACK)]
+            planes = [loads.tile([P, S], F32, name="h0_%d" % t, offset=57344 + 4 * S * t) if b == 0
+                      else keep.tile([P, S], F32, name="h%d_%d" % (b, t)) for t in range(PACK)]
             for step, (t, half) in enumerate(order):
-                acc = psum.tile([P, BANK], F32, name="h_acc", tag="acc" if step < PACK else "y")
+                acc = psum.tile([P, BANK], F32, name="h_acc", tag="bank%d" % step)
                 nc.tensor.matmul_mx(
                     out=acc[:], lhsT=wr_w[b][:, 2 * P * t : 2 * P * (t + 1)].bitcast(FP4X4),
                     lhsT_scale=wr_p[b][:, P * t : P * (t + 1)],
@@ -133,27 +147,11 @@ def tile_list_event_graph_forecast_kernel(
                 nc.scalar.copy(planes[t][:, BANK * half : BANK * (half + 1)], acc[:])
             return planes
 
-        def magnitudes(b):
-            codes, scales, first = wt_q[b]
-            for t in range(PACK):
-                cols = slice(first + P * t, first + P * (t + 1))
-                acc = psum.tile([P, BANK], F32, name="angle", tag="y" if b == 1 else "acc")
-                nc.tensor.matmul_mx(
-                    out=acc[:], lhsT=codes[:, cols].bitcast(FP8X4), lhsT_scale=scales[:, cols],
-                    rhs=early_q[0][:, 0:M].bitcast(FP8X4), rhs_scale=early_q[1][:, 0:M], start=True, stop=True)
-                nc.scalar.activation(out=size(b, 1)[:, t, :], in_=acc[:], func=ACT.Abs, bias=phase_sb[:, b, t : t + 1])
-
         def pick(b, planes):
             x = keep.tile([P, PACK, M], F32, name="x%d" % b)
             for t in range(PACK):
                 nc.vector.tensor_tensor(x[:, t, :], planes[t][:].indirect(idx2[:]), wgt_sb[:], ALU.mult)
             return x
-
-        def cosine(first, count, lo, width):
-            cos = keep.tile([P, PACK * count, width], F32, name="cos%d_%d" % (first, lo))
-            nc.scalar.activation(out=cos[:], in_=size(first, count)[:, :, lo : lo + width],
-                                 func=ACT.Sin, bias=half_pi[:], scale=-1.0)
-            return cos
 
         def modulate(b, cos, lo, width):
             z = keep.tile([P, PACK * width], BF16, name="z%d_%d" % (b, lo), align_bytes=64)
@@ -175,10 +173,9 @@ def tile_list_event_graph_forecast_kernel(
         by_plane = [(t, half) for t in range(PACK) for half in range(2)]
         early = keep.tile([P, 2, PACK * BANK], BF16, name="early", align_bytes=64)
         late = keep.tile([P, 2, PACK * BANK], BF16, name="late", align_bytes=64)
+        group_tf(0)
         planes = [project(0, by_half)]
-        nc.scalar.copy(
-            early[:, 0, :].rearrange("p (c e j) -> p c j e", j=PACK, e=4),
-            tf_raw[:].rearrange("p j (c e) -> p c j e", e=4))
+        group_tf(1)
         planes.append(project(1, by_plane))
         group_wt(1, late[:, 0, :], nc.scalar.copy, 0, SHARE)
         planes.append(project(2, by_plane))
@@ -195,62 +192,80 @@ def tile_list_event_graph_forecast_kernel(
         nc.scalar.mul(half_bf[:], bf_sb[:], 0.5)
         nc.scalar.mul(half_sev[:], sev_sb[:], 0.5)
 
-        size_first = loads.tile([P, PACK, M], F32, name="size_first", offset=0)
-        size_rest = loads.tile([P, (BLOCKS - 1) * PACK, M], F32, name="size_rest", offset=24576)
+        def magnitudes(b, lo, width, offset, first_bank):
+            codes, scales, first = wt_q[b]
+            size = loads.tile([P, PACK, width], F32, name="size%d_%d" % (b, lo), offset=offset)
+            side = BANK // width
+            for k in range(PACK // side):
+                acc = psum.tile([P, side, width], F32, name="angle", tag="bank%d" % (first_bank + k))
+                for t in range(side * k, side * (k + 1)):
+                    cols = slice(first + P * t, first + P * (t + 1))
+                    nc.tensor.matmul_mx(
+                        out=acc[:, t % side, :], lhsT=codes[:, cols].bitcast(FP8X4), lhsT_scale=scales[:, cols],
+                        rhs=early_q[0][:, lo : lo + width].bitcast(FP8X4), rhs_scale=early_q[1][:, lo : lo + width],
+                        start=True, stop=True)
+                for t in range(side * k, side * (k + 1)):
+                    nc.scalar.activation(out=size[:, t, :], in_=acc[:, t % side, :], func=ACT.Abs, bias=phase_sb[:, b, t : t + 1])
+            return size
 
-        def size(first, count):
-            if first == 0:
-                return size_first[:]
-            return size_rest[:, PACK * (first - 1) : PACK * (first - 1 + count), :]
+        def cosine(b, size, lo, width):
+            cos = keep.tile([P, PACK, width], F32, name="cos%d_%d" % (b, lo))
+            nc.scalar.activation(out=cos[:], in_=size, func=ACT.Sin, bias=half_pi[:], scale=-1.0)
+            return cos
 
-        magnitudes(0)
-        cos_first = cosine(0, 1, 0, M)
-        z_halves = [modulate(0, cos_first[:, :, lo : lo + HALF], lo, HALF) for lo in (0, HALF)]
-        z_first = [quantise(z_halves[i][:], HALF, "z0_%d" % i) for i in range(2)]
-        lead = []
+        AT = {(0, 0): 0, (1, 0): 24576, (2, 0): 28672, (1, HALF): 32768, (2, HALF): 36864}
+        size0 = magnitudes(0, 0, M, AT[0, 0], 0)
+        cos = {(0, 0): cosine(0, size0[:, :, 0:HALF], 0, HALF)}
         for b in range(1, BLOCKS):
-            magnitudes(b)
-            lead.append(cosine(b, 1, *PIECES[0])[:])
+            cos[b, 0] = cosine(b, magnitudes(b, 0, HALF, AT[b, 0], 2 + 2 * b)[:], 0, HALF)
+        cos[0, HALF] = cosine(0, size0[:, :, HALF:M], HALF, HALF)
+        cos[1, HALF] = cosine(1, magnitudes(1, HALF, HALF, AT[1, HALF], 0)[:], HALF, HALF)
+        last = magnitudes(2, HALF, HALF, AT[2, HALF], 2)
+        cos[2, HALF] = cosine(2, last[:, :, 0:QUARTER], HALF, QUARTER)
+        cos[2, HALF + QUARTER] = cosine(2, last[:, :, QUARTER:HALF], HALF + QUARTER, QUARTER)
+
+        steps = [(0, 0, HALF), (1, 0, HALF), (2, 0, HALF), (0, HALF, HALF), (1, HALF, HALF),
+                 (2, HALF, QUARTER), (2, HALF + QUARTER, QUARTER)]
+        homes = [AT[1, 0], AT[2, 0], AT[0, 0], AT[1, HALF], AT[2, HALF], AT[2, HALF] + 4 * HALF, None]
+        z_q = {}
+        z = [modulate(0, cos[0, 0][:], 0, HALF)]
+        for i, (b, lo, width) in enumerate(steps):
+            if i + 1 < len(steps):
+                nb, nlo, nwidth = steps[i + 1]
+                z.append(modulate(nb, cos[nb, nlo][:], nlo, nwidth))
+            z_q[b, lo] = quantise(z[i][:], width, "z%d_%d" % (b, lo), homes[i])
 
         types = N // P
         out_v = out.rearrange("(u p) m -> p u m", p=P)
 
-        rest = [lead]
-        for lo, width in PIECES[1:]:
-            both = cosine(1, BLOCKS - 1, lo, width)
-            rest.append([both[:, PACK * i : PACK * (i + 1), :] for i in range(BLOCKS - 1)])
-
-        def prepare(piece):
+        def forecast(piece, first_bank):
             lo, width = PIECES[piece]
-            cos = rest[piece]
-            z = [modulate(b, cos[b - 1], lo, width) for b in range(1, BLOCKS)]
-            return [quantise(z[b - 1][:], width, "z%d_%d" % (b, lo)) for b in range(1, BLOCKS)]
-
-        def forecast(piece, z_q):
-            lo, width = PIECES[piece]
-            cols = slice(lo, lo + width)
-            within = slice(lo % HALF, lo % HALF + width)
-            operands = [(z_first[lo // HALF][0][:, within], z_first[lo // HALF][1][:, within])] + [(c[:], s[:]) for c, s in z_q]
-            accs = [psum.tile([P, width], F32, name="y%d_%d" % (piece, u), tag="y" if piece % 2 else "acc") for u in range(types)]
+            side = BANK // width
+            accs = [psum.tile([P, side, width], F32, name="y%d_%d" % (piece, k), tag="bank%d" % (first_bank + k))
+                    for k in range(types // side)]
             for b in range(BLOCKS):
+                start = lo if (b, lo) in z_q else HALF
+                codes, scales = z_q[b, start]
+                within = slice(lo - start, lo - start + width)
                 for u in range(types):
                     nc.tensor.matmul_mx(
-                        out=accs[u][:], lhsT=wf_w[:, b, P * u : P * (u + 1)].bitcast(FP8X4),
+                        out=accs[u // side][:, u % side, :], lhsT=wf_w[:, b, P * u : P * (u + 1)].bitcast(FP8X4),
                         lhsT_scale=wf_s[:, b, P * u : P * (u + 1)],
-                        rhs=operands[b][0].bitcast(FP8X4), rhs_scale=operands[b][1],
-                        start=(b == 0), stop=(b == BLOCKS - 1))
+                        rhs=codes[:, within].bitcast(FP8X4), rhs_scale=scales[:, within],
+                        start=(b == 0 and u % side == 0), stop=(b == BLOCKS - 1 and u % side == side - 1))
+            if piece == 0:
+                tanh = loads.tile([P, types, width], F32, name="tanh0", offset=AT[2, HALF] + 6 * HALF)
+            else:
+                tanh = keep.tile([P, types, width], F32, name="tanh%d" % piece)
             group = 1 if piece == len(PIECES) - 1 else types
             for first in range(0, types, group):
                 res = keep.tile([P, group, width], F32, name="res%d_%d" % (piece, first))
                 for u in range(first, first + group):
-                    tanh = loads.tile([P, width], F32, name="tanh%d_%d" % (piece, u), offset=24576 + 4 * (M * u + lo))
-                    nc.scalar.activation(out=tanh[:], in_=accs[u][:], func=ACT.Tanh, bias=half_bf[:, u : u + 1], scale=0.5)
-                    nc.vector.tensor_scalar(res[:, u - first, :], tanh[:], half_sev[:, u : u + 1], half_sev[:, u : u + 1], ALU.mult, ALU.add)
-                nc.sync.dma_start(out_v[:, first : first + group, cols], res[:])
+                    nc.scalar.activation(out=tanh[:, u, :], in_=accs[u // side][:, u % side, :], func=ACT.Tanh,
+                                         bias=half_bf[:, u : u + 1], scale=0.5)
+                    nc.vector.tensor_scalar(res[:, u - first, :], tanh[:, u, :], half_sev[:, u : u + 1], half_sev[:, u : u + 1], ALU.mult, ALU.add)
+                nc.sync.dma_start(out_v[:, first : first + group, lo : lo + width], res[:])
 
-        ahead = prepare(0)
-        for piece in range(len(PIECES)):
-            z_q = ahead
-            if piece + 1 < len(PIECES):
-                ahead = prepare(piece + 1)
-            forecast(piece, z_q)
+        forecast(0, 4)
+        forecast(1, 6)
+        forecast(2, 7)

@@ -23,7 +23,8 @@ BLOCKS = H // (P * PACK)
 BANK = 512
 HALF = M // 2
 QUARTER = M // 4
-SHARE = 64
+SHARE = 96
+STORES = [[(0, 1), (1, 1), (2, 1), (3, 1)], [(0, 4)], [(0, 2), (2, 1), (3, 1)]]
 PIECES = [(0, HALF), (HALF, QUARTER), (HALF + QUARTER, QUARTER)]
 
 
@@ -57,7 +58,8 @@ def tile_list_event_graph_forecast_kernel(
         sev_sb = loads.tile([P, N // P], F32, name="sev_sb", offset=20608)
         tf_raw = [loads.tile([P, PACK, S], F32, name="tf_raw0", offset=57344)[:, :, 0:HALF],
                   loads.tile([P, PACK, HALF], F32, name="tf_raw1", offset=24576)[:]]
-        wt_raw = [loads.tile([P, PACK, BANK], F32, name="wt_raw%d" % b, offset=32768 + 8192 * b) for b in range(BLOCKS)]
+        wt_raw = [loads.tile([P, PACK, BANK], F32, name="wt_raw%d" % b, offset=32768 + 8192 * b) for b in range(1, BLOCKS)]
+        wt_first = [loads.tile([P, PACK, HALF], F32, name="wt_first%d" % i, offset=32768 + 4096 * i) for i in range(2)]
 
         nc.gpsimd.memset(tab_s[:].bitcast(I32), 0)
         nc.vector.memset(wr_s[:].bitcast(I32), 0)
@@ -71,7 +73,10 @@ def tile_list_event_graph_forecast_kernel(
                 nc.sync.dma_start(plane[32 * q : 32 * q + 4].bitcast(I32), rows[4 * q : 4 * q + 4].bitcast(I32))
 
         def load_wt(b):
-            nc.sync.dma_start(wt_raw[b][:], wt[:, BANK * b : BANK * (b + 1)].rearrange("(p j) c -> p j c", j=PACK))
+            nc.sync.dma_start(wt_raw[b - 1][:], wt[:, BANK * b : BANK * (b + 1)].rearrange("(p j) c -> p j c", j=PACK))
+
+        def load_wt_first(i):
+            nc.sync.dma_start(wt_first[i][:], wt[:, HALF * i : HALF * (i + 1)].rearrange("(p j) c -> p j c", j=PACK))
 
         def load_tf(i):
             nc.sync.dma_start(tf_raw[i], tf[:, HALF * i : HALF * (i + 1)].rearrange("(p j) m -> p j m", j=PACK))
@@ -88,8 +93,9 @@ def tile_list_event_graph_forecast_kernel(
         nc.sync.dma_start(tab_w[:].bitcast(I32), tab_words[0].rearrange("p t i -> p (t i)").bitcast(I32))
         load_scale_rows(wr_s, wr_scales[0])
         load_tf(0)
+        load_wt_first(0)
         nc.sync.dma_start(wr_rest[:].bitcast(I32), wr_words[0, :, 4 * BANK :].bitcast(I32))
-        load_wt(0)
+        load_wt_first(1)
         nc.sync.dma_start(wgt_sb[:], wgt)
         load_tf(1)
         nc.sync.dma_start(phase_sb[:], phase.rearrange("(b p i) -> p b i", b=BLOCKS, i=PACK))
@@ -132,7 +138,12 @@ def tile_list_event_graph_forecast_kernel(
 
         def group_wt(b, grouped, copy, lo=0, hi=P):
             copy(grouped.rearrange("p (t c j) -> p c j t", t=PACK, j=PACK)[:, lo:hi],
-                 wt_raw[b][:].rearrange("p j (c t) -> p c j t", t=PACK)[:, lo:hi])
+                 wt_raw[b - 1][:].rearrange("p j (c t) -> p c j t", t=PACK)[:, lo:hi])
+
+        def group_wt_first(i):
+            nc.vector.tensor_copy(
+                early[:, 1, :].rearrange("p (t c j) -> p c j t", t=PACK, j=PACK)[:, 64 * i : 64 * (i + 1)],
+                wt_first[i][:].rearrange("p j (c t) -> p c j t", t=PACK))
 
         def project(b, order):
             planes = [loads.tile([P, S], F32, name="h0_%d" % t, offset=57344 + 4 * S * t) if b == 0
@@ -148,7 +159,10 @@ def tile_list_event_graph_forecast_kernel(
             return planes
 
         def pick(b, planes):
-            x = keep.tile([P, PACK, M], F32, name="x%d" % b)
+            if b == BLOCKS - 1:
+                x = loads.tile([P, PACK, M], F32, name="x_last", offset=49152)
+            else:
+                x = keep.tile([P, PACK, M], F32, name="x%d" % b)
             for t in range(PACK):
                 nc.vector.tensor_tensor(x[:, t, :], planes[t][:].indirect(idx2[:]), wgt_sb[:], ALU.mult)
             return x
@@ -180,7 +194,8 @@ def tile_list_event_graph_forecast_kernel(
         group_wt(1, late[:, 0, :], nc.scalar.copy, 0, SHARE)
         planes.append(project(2, by_plane))
 
-        group_wt(0, early[:, 1, :], nc.vector.tensor_copy)
+        group_wt_first(0)
+        group_wt_first(1)
         x = [pick(0, planes[0])]
         early_q = quantise(early[:].rearrange("p a c -> p (a c)"), 2 * BANK, "early")
         group_wt(1, late[:, 0, :], nc.vector.tensor_copy, SHARE, P)
@@ -257,8 +272,7 @@ def tile_list_event_graph_forecast_kernel(
                 tanh = loads.tile([P, types, width], F32, name="tanh0", offset=AT[2, HALF] + 6 * HALF)
             else:
                 tanh = keep.tile([P, types, width], F32, name="tanh%d" % piece)
-            group = 1 if piece == len(PIECES) - 1 else types
-            for first in range(0, types, group):
+            for first, group in STORES[piece]:
                 res = keep.tile([P, group, width], F32, name="res%d_%d" % (piece, first))
                 for u in range(first, first + group):
                     nc.scalar.activation(out=tanh[:, u, :], in_=accs[u // side][:, u % side, :], func=ACT.Tanh,

@@ -23,7 +23,7 @@ BLOCKS = H // (P * PACK)
 BANK = 512
 HALF = M // 2
 QUARTER = M // 4
-SHARE = 96
+SHARE = 112
 STORES = [[(0, 1), (1, 1), (2, 1), (3, 1)], [(0, 4)], [(0, 2), (2, 1), (3, 1)]]
 PIECES = [(0, HALF), (HALF, QUARTER), (HALF + QUARTER, QUARTER)]
 
@@ -241,7 +241,7 @@ def tile_list_event_graph_forecast_kernel(
 
         steps = [(0, 0, HALF), (1, 0, HALF), (2, 0, HALF), (0, HALF, HALF), (1, HALF, HALF),
                  (2, HALF, QUARTER), (2, HALF + QUARTER, QUARTER)]
-        homes = [AT[1, 0], AT[2, 0], AT[0, 0], AT[1, HALF], AT[2, HALF], AT[2, HALF] + 4 * HALF, None]
+        homes = [AT[1, 0], AT[2, 0], AT[0, 0], AT[1, HALF], None, AT[2, HALF], None]
         z_q = {}
         z = [modulate(0, cos[0, 0][:], 0, HALF)]
         for i, (b, lo, width) in enumerate(steps):
@@ -253,33 +253,36 @@ def tile_list_event_graph_forecast_kernel(
         types = N // P
         out_v = out.rearrange("(u p) m -> p u m", p=P)
 
-        def forecast(piece, first_bank):
+        def forecast(piece, banks):
             lo, width = PIECES[piece]
-            side = BANK // width
-            accs = [psum.tile([P, side, width], F32, name="y%d_%d" % (piece, k), tag="bank%d" % (first_bank + k))
-                    for k in range(types // side)]
+            sums, opens, closes = [], [], []
+            for bank, count in banks:
+                acc = psum.tile([P, count, width], F32, name="y%d_%d" % (piece, bank), tag="bank%d" % bank)
+                sums.extend(acc[:, i, :] for i in range(count))
+                opens.extend(i == 0 for i in range(count))
+                closes.extend(i == count - 1 for i in range(count))
             for b in range(BLOCKS):
                 start = lo if (b, lo) in z_q else HALF
                 codes, scales = z_q[b, start]
                 within = slice(lo - start, lo - start + width)
                 for u in range(types):
                     nc.tensor.matmul_mx(
-                        out=accs[u // side][:, u % side, :], lhsT=wf_w[:, b, P * u : P * (u + 1)].bitcast(FP8X4),
+                        out=sums[u], lhsT=wf_w[:, b, P * u : P * (u + 1)].bitcast(FP8X4),
                         lhsT_scale=wf_s[:, b, P * u : P * (u + 1)],
                         rhs=codes[:, within].bitcast(FP8X4), rhs_scale=scales[:, within],
-                        start=(b == 0 and u % side == 0), stop=(b == BLOCKS - 1 and u % side == side - 1))
+                        start=(b == 0 and opens[u]), stop=(b == BLOCKS - 1 and closes[u]))
             if piece == 0:
-                tanh = loads.tile([P, types, width], F32, name="tanh0", offset=AT[2, HALF] + 6 * HALF)
+                tanh = loads.tile([P, types, width], F32, name="tanh0", offset=AT[2, HALF] + 2 * HALF)
             else:
                 tanh = keep.tile([P, types, width], F32, name="tanh%d" % piece)
             for first, group in STORES[piece]:
                 res = keep.tile([P, group, width], F32, name="res%d_%d" % (piece, first))
                 for u in range(first, first + group):
-                    nc.scalar.activation(out=tanh[:, u, :], in_=accs[u // side][:, u % side, :], func=ACT.Tanh,
+                    nc.scalar.activation(out=tanh[:, u, :], in_=sums[u], func=ACT.Tanh,
                                          bias=half_bf[:, u : u + 1], scale=0.5)
                     nc.vector.tensor_scalar(res[:, u - first, :], tanh[:, u, :], half_sev[:, u : u + 1], half_sev[:, u : u + 1], ALU.mult, ALU.add)
                 nc.sync.dma_start(out_v[:, first : first + group, lo : lo + width], res[:])
 
-        forecast(0, 4)
-        forecast(1, 6)
-        forecast(2, 7)
+        forecast(0, [(4, 2), (5, 2)])
+        forecast(1, [(0, 1), (1, 1), (6, 2)])
+        forecast(2, [(2, 1), (3, 1), (7, 2)])

@@ -23,7 +23,7 @@ BLOCKS = H // (P * PACK)
 BANK = 512
 HALF = M // 2
 QUARTER = M // 4
-SHARE = 112
+SHARE = 80
 STORES = [[(0, 1), (1, 1), (2, 1), (3, 1)], [(0, 4)], [(0, 2), (2, 1), (3, 1)]]
 PIECES = [(0, HALF), (HALF, QUARTER), (HALF + QUARTER, QUARTER)]
 
@@ -43,8 +43,8 @@ def tile_list_event_graph_forecast_kernel(
         tab_s = keep.tile([P, T], U8, name="tab_s", align_bytes=64)
         wr_s = loads.tile([P, H], U8, name="wr_s", align_bytes=64, offset=73728)
         wf_s = keep.tile([P, BLOCKS, N], U8, name="wf_s", align_bytes=64)
-        half_bf = keep.tile([P, N // P], F32, name="half_bf")
-        half_sev = keep.tile([P, N // P], F32, name="half_sev")
+        halves = keep.tile([P, 2, N // P], F32, name="halves")
+        half_bf, half_sev = halves[:, 0, :], halves[:, 1, :]
         half_pi = keep.tile([P, 1], F32, name="half_pi")
         warm = keep.tile([P, 1], F32, name="warm")
         one = loads.tile([P, 18432], F32, name="one", offset=0)
@@ -54,8 +54,7 @@ def tile_list_event_graph_forecast_kernel(
         wf_w = loads.tile([P, BLOCKS, N], U32, name="wf_w", align_bytes=64, offset=12288)
         wgt_sb = loads.tile([P, M], F32, name="wgt_sb", offset=18432)
         phase_sb = loads.tile([P, BLOCKS, PACK], F32, name="phase_sb", offset=20480)
-        bf_sb = loads.tile([P, N // P], F32, name="bf_sb", offset=20544)
-        sev_sb = loads.tile([P, N // P], F32, name="sev_sb", offset=20608)
+        ends = loads.tile([P, 2, 8], F32, name="ends", offset=20544)
         tf_raw = [loads.tile([P, PACK, S], F32, name="tf_raw0", offset=57344)[:, :, 0:HALF],
                   loads.tile([P, PACK, HALF], F32, name="tf_raw1", offset=24576)[:]]
         wt_raw = [loads.tile([P, PACK, BANK], F32, name="wt_raw%d" % b, offset=32768 + 8192 * b) for b in range(1, BLOCKS)]
@@ -94,8 +93,8 @@ def tile_list_event_graph_forecast_kernel(
         load_scale_rows(wr_s, wr_scales[0])
         load_tf(0)
         load_wt_first(0)
-        nc.sync.dma_start(wr_rest[:].bitcast(I32), wr_words[0, :, 4 * BANK :].bitcast(I32))
         load_wt_first(1)
+        nc.sync.dma_start(wr_rest[:].bitcast(I32), wr_words[0, :, 4 * BANK :].bitcast(I32))
         nc.sync.dma_start(wgt_sb[:], wgt)
         load_tf(1)
         nc.sync.dma_start(phase_sb[:], phase.rearrange("(b p i) -> p b i", b=BLOCKS, i=PACK))
@@ -104,23 +103,22 @@ def tile_list_event_graph_forecast_kernel(
         nc.sync.dma_start(wf_w[:].bitcast(I32), wf_words.rearrange("a p c i -> p a (c i)").bitcast(I32))
         load_scale_rows(wf_s, wf_scales.rearrange("a r c -> r a c"))
         with nc.allow_non_contiguous_dma(reason="one value a partition"):
-            nc.sync.dma_start(bf_sb[:], bf.rearrange("(u p) -> p u", p=P))
-            nc.sync.dma_start(sev_sb[:], sev.rearrange("(u p) -> p u", p=P))
+            nc.sync.dma_start(ends[:, 0, 0 : N // P], bf.rearrange("(u p) -> p u", p=P))
+            nc.sync.dma_start(ends[:, 1, 0 : N // P], sev.rearrange("(u p) -> p u", p=P))
 
-        def deal_words(b):
-            raw = wr_rest[:] if b == BLOCKS - 1 else wr_first[:, 2 * BANK * b : 2 * BANK * (b + 1)]
-            words = keep.tile([P, 2 * BANK], U8, name="wr_wp%d" % b, align_bytes=64)
+        def deal_words(raw, count, name):
+            words = keep.tile([P, count * 2 * BANK], U8, name=name, align_bytes=64)
             nc.vector.tensor_copy(
-                words[:].bitcast(U16).rearrange("p (t c) -> p c t", t=PACK),
-                raw.bitcast(U16).rearrange("p (c t) -> p c t", t=PACK))
-            return words
+                words[:].bitcast(U16).rearrange("p (b t c) -> p b c t", b=count, t=PACK),
+                raw[:].bitcast(U16).rearrange("p (b c t) -> p b c t", b=count, t=PACK))
+            return [words[:, 2 * BANK * i : 2 * BANK * (i + 1)] for i in range(count)]
 
-        def deal_scales(b):
-            scales = keep.tile([P, BANK], U8, name="wr_sp%d" % b, align_bytes=64)
+        def deal_scales(first, count):
+            scales = keep.tile([P, count * BANK], U8, name="wr_sp%d" % first, align_bytes=64)
             nc.vector.tensor_copy(
-                scales[:].rearrange("p (t c) -> p c t", t=PACK),
-                wr_s[:, BANK * b : BANK * (b + 1)].rearrange("p (c t) -> p c t", t=PACK))
-            return scales
+                scales[:].rearrange("p (b t c) -> p b c t", b=count, t=PACK),
+                wr_s[:, BANK * first : BANK * (first + count)].rearrange("p (b c t) -> p b c t", b=count, t=PACK))
+            return [scales[:, BANK * i : BANK * (i + 1)] for i in range(count)]
 
         def gather_words(half):
             picked = loads.tile([P, BANK], U32, name="v_w%d" % half, align_bytes=64, offset=75776 - 2048 * half)
@@ -175,37 +173,46 @@ def tile_list_event_graph_forecast_kernel(
                 cos.rearrange("p t (c e) -> p c t e", e=2), ALU.mult)
             return z
 
-        wr_w = [deal_words(b) for b in range(BLOCKS - 1)]
+        wr_w = deal_words(wr_first, BLOCKS - 1, "wr_wp0")
         v_s = keep.tile([P, S], U8, name="v_s", align_bytes=64)
         nc.vector.tensor_copy(v_s[:], tab_s[:].indirect(idx[:]))
         v_w = [gather_words(0)]
-        wr_p = [deal_scales(b) for b in range(BLOCKS)]
+        wr_p = deal_scales(0, 1) + deal_scales(1, BLOCKS - 1)
         v_w.append(gather_words(1))
-        wr_w.append(deal_words(BLOCKS - 1))
 
         by_half = [(t, half) for half in range(2) for t in range(PACK)]
         by_plane = [(t, half) for t in range(PACK) for half in range(2)]
         early = keep.tile([P, 2, PACK * BANK], BF16, name="early", align_bytes=64)
         late = keep.tile([P, 2, PACK * BANK], BF16, name="late", align_bytes=64)
+        early_q = (keep.tile([P, 2 * BANK], U32, name="early_codes", align_bytes=64),
+                   keep.tile([P, 2 * BANK], U8, name="early_scales", align_bytes=64))
+
+        def quantise_early(lo, width):
+            nc.vector.quantize_mx(
+                out=early_q[0][:, lo : lo + width].bitcast(FP8X4), scales=early_q[1][:, lo : lo + width],
+                in_=early[:].rearrange("p a c -> p (a c)")[:, PACK * lo : PACK * (lo + width)])
+
         group_tf(0)
+        quantise_early(0, HALF)
+        group_wt_first(0)
+        group_wt_first(1)
+        wr_w = wr_w + deal_words(wr_rest, 1, "wr_wp2")
+        quantise_early(BANK, BANK)
         planes = [project(0, by_half)]
         group_tf(1)
         planes.append(project(1, by_plane))
         group_wt(1, late[:, 0, :], nc.scalar.copy, 0, SHARE)
         planes.append(project(2, by_plane))
 
-        group_wt_first(0)
-        group_wt_first(1)
         x = [pick(0, planes[0])]
-        early_q = quantise(early[:].rearrange("p a c -> p (a c)"), 2 * BANK, "early")
+        quantise_early(HALF, HALF)
         group_wt(1, late[:, 0, :], nc.vector.tensor_copy, SHARE, P)
         group_wt(2, late[:, 1, :], nc.vector.tensor_copy)
         x.append(pick(1, planes[1]))
         late_q = quantise(late[:].rearrange("p a c -> p (a c)"), 2 * BANK, "late")
         x.append(pick(2, planes[2]))
         wt_q = [early_q + (BANK,), late_q + (0,), late_q + (BANK,)]
-        nc.scalar.mul(half_bf[:], bf_sb[:], 0.5)
-        nc.scalar.mul(half_sev[:], sev_sb[:], 0.5)
+        nc.scalar.mul(halves[:], ends[:, :, 0 : N // P], 0.5)
 
         def magnitudes(b, lo, width, offset, first_bank):
             codes, scales, first = wt_q[b]

@@ -19,13 +19,33 @@ ALU = mybir.AluOpType
 
 P = 128
 PACK = 4
-BLOCKS = H // (P * PACK)
+GROUPS = H // (P * PACK)
+LAST = GROUPS - 1
 BANK = 512
+TYPE_TILES = N // P
 HALF = M // 2
 QUARTER = M // 4
-SHARE = 80
-STORES = [[(0, 1), (1, 1), (2, 1), (3, 1)], [(0, 4)], [(0, 2), (2, 1), (3, 1)]]
+
+SCALAR_SHARE = 64
+
 PIECES = [(0, HALF), (HALF, QUARTER), (HALF + QUARTER, QUARTER)]
+STORES = [[(0, 1), (1, 1), (2, 1), (3, 1)], [(0, 4)], [(0, 2), (2, 1), (3, 1)]]
+SUM_BANKS = [[(4, 2), (5, 2)], [(0, 1), (1, 1), (6, 2)], [(2, 1), (3, 1), (7, 2)]]
+
+KIB = 1024
+AT_TAB_W = 0
+AT_WR_REST = 9 * KIB
+AT_WF_W = 12 * KIB
+AT_WGT = 18 * KIB
+AT_PHASE = 20 * KIB
+AT_ENDS = AT_PHASE + 64
+AT_TF_SECOND = 24 * KIB
+AT_SPARE = 28 * KIB
+AT_WT = 32 * KIB
+AT_TF_FIRST = 56 * KIB
+AT_WR_S = 72 * KIB
+AT_V_W = 74 * KIB
+AT_SIZE = {(0, 0): AT_TAB_W, (1, 0): AT_TF_SECOND, (2, 0): AT_SPARE, (1, HALF): AT_WT, (2, HALF): AT_WT + 4 * KIB}
 
 
 def tile_list_event_graph_forecast_kernel(
@@ -35,30 +55,32 @@ def tile_list_event_graph_forecast_kernel(
     nc = tc.nc
     with ExitStack() as ctx:
         keep = ctx.enter_context(tc.tile_pool(name="keep", bufs=1))
-        loads = ctx.enter_context(tc.tile_pool(name="loads", bufs=1))
+        staged = ctx.enter_context(tc.tile_pool(name="loads", bufs=1))
         psum = ctx.enter_context(tc.psum_pool(name="psum", bufs=1))
 
         idx = keep.tile([P, S // 16], U16, name="idx")
         idx2 = keep.tile([P, M // 16], U16, name="idx2")
         tab_s = keep.tile([P, T], U8, name="tab_s", align_bytes=64)
-        wr_s = loads.tile([P, H], U8, name="wr_s", align_bytes=64, offset=73728)
-        wf_s = keep.tile([P, BLOCKS, N], U8, name="wf_s", align_bytes=64)
-        halves = keep.tile([P, 2, N // P], F32, name="halves")
-        half_bf, half_sev = halves[:, 0, :], halves[:, 1, :]
+        wr_s = staged.tile([P, H], U8, name="wr_s", align_bytes=64, offset=AT_WR_S)
+        wf_s = keep.tile([P, GROUPS, N], U8, name="wf_s", align_bytes=64)
+        halved = keep.tile([P, 2, TYPE_TILES], F32, name="halves")
+        half_bf, half_sev = halved[:, 0, :], halved[:, 1, :]
         half_pi = keep.tile([P, 1], F32, name="half_pi")
         warm = keep.tile([P, 1], F32, name="warm")
-        one = loads.tile([P, 18432], F32, name="one", offset=0)
-        tab_w = loads.tile([P, T], U32, name="tab_w", align_bytes=64, offset=0)
-        wr_first = keep.tile([P, 4 * BANK], U8, name="wr_first", align_bytes=64)
-        wr_rest = loads.tile([P, 2 * BANK], U8, name="wr_rest", align_bytes=64, offset=9216)
-        wf_w = loads.tile([P, BLOCKS, N], U32, name="wf_w", align_bytes=64, offset=12288)
-        wgt_sb = loads.tile([P, M], F32, name="wgt_sb", offset=18432)
-        phase_sb = loads.tile([P, BLOCKS, PACK], F32, name="phase_sb", offset=20480)
-        ends = loads.tile([P, 2, 8], F32, name="ends", offset=20544)
-        tf_raw = [loads.tile([P, PACK, S], F32, name="tf_raw0", offset=57344)[:, :, 0:HALF],
-                  loads.tile([P, PACK, HALF], F32, name="tf_raw1", offset=24576)[:]]
-        wt_raw = [loads.tile([P, PACK, BANK], F32, name="wt_raw%d" % b, offset=32768 + 8192 * b) for b in range(1, BLOCKS)]
-        wt_first = [loads.tile([P, PACK, HALF], F32, name="wt_first%d" % i, offset=32768 + 4096 * i) for i in range(2)]
+        one = staged.tile([P, AT_WR_S // 4], F32, name="one", offset=0)
+        tab_w = staged.tile([P, T], U32, name="tab_w", align_bytes=64, offset=AT_TAB_W)
+        wr_first = keep.tile([P, 2 * BANK * LAST], U8, name="wr_first", align_bytes=64)
+        wr_rest = staged.tile([P, 2 * BANK], U8, name="wr_rest", align_bytes=64, offset=AT_WR_REST)
+        wf_w = staged.tile([P, GROUPS, N], U32, name="wf_w", align_bytes=64, offset=AT_WF_W)
+        wgt_sb = staged.tile([P, M], F32, name="wgt_sb", offset=AT_WGT)
+        phase_sb = staged.tile([P, GROUPS, PACK], F32, name="phase_sb", offset=AT_PHASE)
+        ends = staged.tile([P, 2, 8], F32, name="ends", offset=AT_ENDS)
+        tf_raw = [staged.tile([P, PACK, S], F32, name="tf_raw0", offset=AT_TF_FIRST)[:, :, 0:HALF],
+                  staged.tile([P, PACK, HALF], F32, name="tf_raw1", offset=AT_TF_SECOND)[:]]
+        wt_raw = {b: staged.tile([P, PACK, BANK], F32, name="wt_raw%d" % b, offset=AT_WT + 8 * KIB * b)
+                  for b in range(1, GROUPS)}
+        wt_first = [staged.tile([P, PACK, BANK // 2], F32, name="wt_first%d" % i, offset=AT_WT + 4 * KIB * i)
+                    for i in range(2)]
 
         nc.gpsimd.memset(tab_s[:].bitcast(I32), 0)
         nc.vector.memset(wr_s[:].bitcast(I32), 0)
@@ -67,229 +89,215 @@ def tile_list_event_graph_forecast_kernel(
         nc.scalar.activation(out=warm[:], in_=half_pi[:], func=ACT.Silu)
         nc.gpsimd.memset(wf_s[:].rearrange("p a c -> p (a c)").bitcast(I32), 0)
 
-        def load_scale_rows(plane, rows):
+        def load_scale_rows(scale_tile, rows):
             for q in range(4):
-                nc.sync.dma_start(plane[32 * q : 32 * q + 4].bitcast(I32), rows[4 * q : 4 * q + 4].bitcast(I32))
+                nc.sync.dma_start(scale_tile[32 * q : 32 * q + 4].bitcast(I32), rows[4 * q : 4 * q + 4].bitcast(I32))
 
-        def load_wt(b):
-            nc.sync.dma_start(wt_raw[b - 1][:], wt[:, BANK * b : BANK * (b + 1)].rearrange("(p j) c -> p j c", j=PACK))
+        def load_k_rows(raw, source, col, count):
+            nc.sync.dma_start(raw, source[:, col : col + count].rearrange("(p j) c -> p j c", j=PACK))
 
-        def load_wt_first(i):
-            nc.sync.dma_start(wt_first[i][:], wt[:, HALF * i : HALF * (i + 1)].rearrange("(p j) c -> p j c", j=PACK))
-
-        def load_tf(i):
-            nc.sync.dma_start(tf_raw[i], tf[:, HALF * i : HALF * (i + 1)].rearrange("(p j) m -> p j m", j=PACK))
-
-        def group_tf(i):
-            nc.scalar.copy(
-                early[:, 0, PACK * HALF * i : PACK * HALF * (i + 1)].rearrange("p (c e j) -> p c j e", j=PACK, e=4),
-                tf_raw[i].rearrange("p j (c e) -> p c j e", e=4))
-
-        nc.sync.dma_start(wr_first[:].bitcast(I32), wr_words[0, :, 0 : 4 * BANK].bitcast(I32))
+        nc.sync.dma_start(wr_first[:].bitcast(I32), wr_words[0, :, 0 : 2 * BANK * LAST].bitcast(I32))
         nc.sync.dma_start(idx[:], offs)
         nc.sync.dma_start(idx2[:], offs2)
         load_scale_rows(tab_s, tab_scales[0])
         nc.sync.dma_start(tab_w[:].bitcast(I32), tab_words[0].rearrange("p t i -> p (t i)").bitcast(I32))
         load_scale_rows(wr_s, wr_scales[0])
-        load_tf(0)
-        load_wt_first(0)
-        load_wt_first(1)
-        nc.sync.dma_start(wr_rest[:].bitcast(I32), wr_words[0, :, 4 * BANK :].bitcast(I32))
+        load_k_rows(tf_raw[0], tf, 0, HALF)
+        for i in range(2):
+            load_k_rows(wt_first[i][:], wt, BANK // 2 * i, BANK // 2)
+        nc.sync.dma_start(wr_rest[:].bitcast(I32), wr_words[0, :, 2 * BANK * LAST :].bitcast(I32))
         nc.sync.dma_start(wgt_sb[:], wgt)
-        load_tf(1)
-        nc.sync.dma_start(phase_sb[:], phase.rearrange("(b p i) -> p b i", b=BLOCKS, i=PACK))
-        load_wt(1)
-        load_wt(2)
+        load_k_rows(tf_raw[1], tf, HALF, HALF)
+        nc.sync.dma_start(phase_sb[:], phase.rearrange("(b p i) -> p b i", b=GROUPS, i=PACK))
+        for b in range(1, GROUPS):
+            load_k_rows(wt_raw[b][:], wt, BANK * b, BANK)
         nc.sync.dma_start(wf_w[:].bitcast(I32), wf_words.rearrange("a p c i -> p a (c i)").bitcast(I32))
         load_scale_rows(wf_s, wf_scales.rearrange("a r c -> r a c"))
         with nc.allow_non_contiguous_dma(reason="one value a partition"):
-            nc.sync.dma_start(ends[:, 0, 0 : N // P], bf.rearrange("(u p) -> p u", p=P))
-            nc.sync.dma_start(ends[:, 1, 0 : N // P], sev.rearrange("(u p) -> p u", p=P))
+            nc.sync.dma_start(ends[:, 0, 0:TYPE_TILES], bf.rearrange("(u p) -> p u", p=P))
+            nc.sync.dma_start(ends[:, 1, 0:TYPE_TILES], sev.rearrange("(u p) -> p u", p=P))
 
-        def deal_words(raw, count, name):
-            words = keep.tile([P, count * 2 * BANK], U8, name=name, align_bytes=64)
+        def deal_words(raw, groups, name):
+            words = keep.tile([P, groups * 2 * BANK], U8, name=name, align_bytes=64)
             nc.vector.tensor_copy(
-                words[:].bitcast(U16).rearrange("p (b t c) -> p b c t", b=count, t=PACK),
-                raw[:].bitcast(U16).rearrange("p (b c t) -> p b c t", b=count, t=PACK))
-            return [words[:, 2 * BANK * i : 2 * BANK * (i + 1)] for i in range(count)]
+                words[:].bitcast(U16).rearrange("p (b t c) -> p b c t", b=groups, t=PACK),
+                raw[:].bitcast(U16).rearrange("p (b c t) -> p b c t", b=groups, t=PACK))
+            return [words[:, 2 * BANK * i : 2 * BANK * (i + 1)] for i in range(groups)]
 
-        def deal_scales(first, count):
-            scales = keep.tile([P, count * BANK], U8, name="wr_sp%d" % first, align_bytes=64)
+        def deal_scales(b, groups):
+            scales = keep.tile([P, groups * BANK], U8, name="wr_sp%d" % b, align_bytes=64)
             nc.vector.tensor_copy(
-                scales[:].rearrange("p (b t c) -> p b c t", b=count, t=PACK),
-                wr_s[:, BANK * first : BANK * (first + count)].rearrange("p (b c t) -> p b c t", b=count, t=PACK))
-            return [scales[:, BANK * i : BANK * (i + 1)] for i in range(count)]
+                scales[:].rearrange("p (b t c) -> p b c t", b=groups, t=PACK),
+                wr_s[:, BANK * b : BANK * (b + groups)].rearrange("p (b c t) -> p b c t", b=groups, t=PACK))
+            return [scales[:, BANK * i : BANK * (i + 1)] for i in range(groups)]
 
-        def gather_words(half):
-            picked = loads.tile([P, BANK], U32, name="v_w%d" % half, align_bytes=64, offset=75776 - 2048 * half)
-            nc.vector.tensor_copy(picked[:], tab_w[:].indirect(idx[:, 32 * half : 32 * (half + 1)]))
-            return picked
+        def gather_words(part, offset):
+            words = staged.tile([P, BANK], U32, name="v_w%d" % part, align_bytes=64, offset=offset)
+            nc.vector.tensor_copy(words[:], tab_w[:].indirect(idx[:, BANK // 16 * part : BANK // 16 * (part + 1)]))
+            return words
 
-        def quantise(grouped, width, name, offset=None):
+        def quantise(woven, columns, name, offset=None):
             if offset is None:
-                codes = keep.tile([P, width], U32, name=name + "_codes", align_bytes=64)
+                codes = keep.tile([P, columns], U32, name=name + "_codes", align_bytes=64)
             else:
-                codes = loads.tile([P, width], U32, name=name + "_codes", align_bytes=64, offset=offset)
-            scales = keep.tile([P, width], U8, name=name + "_scales", align_bytes=64)
-            nc.vector.quantize_mx(out=codes[:].bitcast(FP8X4), scales=scales[:], in_=grouped)
+                codes = staged.tile([P, columns], U32, name=name + "_codes", align_bytes=64, offset=offset)
+            scales = keep.tile([P, columns], U8, name=name + "_scales", align_bytes=64)
+            nc.vector.quantize_mx(out=codes[:].bitcast(FP8X4), scales=scales[:], in_=woven)
             return codes, scales
 
-        def group_wt(b, grouped, copy, lo=0, hi=P):
-            copy(grouped.rearrange("p (t c j) -> p c j t", t=PACK, j=PACK)[:, lo:hi],
-                 wt_raw[b - 1][:].rearrange("p j (c t) -> p c j t", t=PACK)[:, lo:hi])
+        def weave_tf(i):
+            nc.scalar.copy(
+                early[:, 0, PACK * HALF * i : PACK * HALF * (i + 1)].rearrange("p (c e j) -> p c j e", j=PACK, e=4),
+                tf_raw[i].rearrange("p j (c e) -> p c j e", e=4))
 
-        def group_wt_first(i):
-            nc.vector.tensor_copy(
-                early[:, 1, :].rearrange("p (t c j) -> p c j t", t=PACK, j=PACK)[:, 64 * i : 64 * (i + 1)],
-                wt_first[i][:].rearrange("p j (c t) -> p c j t", t=PACK))
+        def weave_wt(copy, woven, raw, c_from, c_to, c_raw):
+            copy(woven.rearrange("p (t c j) -> p c j t", t=PACK, j=PACK)[:, c_from:c_to],
+                 raw[:].rearrange("p j (c t) -> p c j t", t=PACK)[:, c_from - c_raw : c_to - c_raw])
 
         def project(b, order):
-            planes = [loads.tile([P, S], F32, name="h0_%d" % t, offset=57344 + 4 * S * t) if b == 0
+            planes = [staged.tile([P, S], F32, name="h0_%d" % t, offset=AT_TF_FIRST + 4 * S * t) if b == 0
                       else keep.tile([P, S], F32, name="h%d_%d" % (b, t)) for t in range(PACK)]
-            for step, (t, half) in enumerate(order):
-                acc = psum.tile([P, BANK], F32, name="h_acc", tag="bank%d" % step)
+            for bank, (t, part) in enumerate(order):
+                acc = psum.tile([P, BANK], F32, name="h_acc", tag="bank%d" % bank)
                 nc.tensor.matmul_mx(
                     out=acc[:], lhsT=wr_w[b][:, 2 * P * t : 2 * P * (t + 1)].bitcast(FP4X4),
                     lhsT_scale=wr_p[b][:, P * t : P * (t + 1)],
-                    rhs=v_w[half][:].bitcast(FP8X4), rhs_scale=v_s[:, BANK * half : BANK * (half + 1)],
+                    rhs=v_w[part][:].bitcast(FP8X4), rhs_scale=v_s[:, BANK * part : BANK * (part + 1)],
                     start=True, stop=True)
-                nc.scalar.copy(planes[t][:, BANK * half : BANK * (half + 1)], acc[:])
+                nc.scalar.copy(planes[t][:, BANK * part : BANK * (part + 1)], acc[:])
             return planes
 
         def pick(b, planes):
-            if b == BLOCKS - 1:
-                x = loads.tile([P, PACK, M], F32, name="x_last", offset=49152)
+            if b == LAST:
+                picked = staged.tile([P, PACK, M], F32, name="x_last", offset=AT_WT + 8 * KIB * LAST)
             else:
-                x = keep.tile([P, PACK, M], F32, name="x%d" % b)
+                picked = keep.tile([P, PACK, M], F32, name="x%d" % b)
             for t in range(PACK):
-                nc.vector.tensor_tensor(x[:, t, :], planes[t][:].indirect(idx2[:]), wgt_sb[:], ALU.mult)
-            return x
+                nc.vector.tensor_tensor(picked[:, t, :], planes[t][:].indirect(idx2[:]), wgt_sb[:], ALU.mult)
+            return picked
 
-        def modulate(b, cos, lo, width):
+        def modulate(b, lo, width):
             z = keep.tile([P, PACK * width], BF16, name="z%d_%d" % (b, lo), align_bytes=64)
             nc.vector.tensor_tensor(
                 z[:].rearrange("p (c e t) -> p c t e", t=PACK, e=2),
                 x[b][:, :, lo : lo + width].rearrange("p t (c e) -> p c t e", e=2),
-                cos.rearrange("p t (c e) -> p c t e", e=2), ALU.mult)
+                cos[b, lo][:].rearrange("p t (c e) -> p c t e", e=2), ALU.mult)
             return z
 
-        wr_w = deal_words(wr_first, BLOCKS - 1, "wr_wp0")
+        wr_w = deal_words(wr_first, LAST, "wr_wp0")
         v_s = keep.tile([P, S], U8, name="v_s", align_bytes=64)
         nc.vector.tensor_copy(v_s[:], tab_s[:].indirect(idx[:]))
-        v_w = [gather_words(0)]
-        wr_p = deal_scales(0, 1) + deal_scales(1, BLOCKS - 1)
-        v_w.append(gather_words(1))
+        v_w = [gather_words(0, AT_V_W)]
+        wr_p = deal_scales(0, 1) + deal_scales(1, LAST)
+        v_w.append(gather_words(1, AT_WR_S))
 
-        by_half = [(t, half) for half in range(2) for t in range(PACK)]
-        by_plane = [(t, half) for t in range(PACK) for half in range(2)]
         early = keep.tile([P, 2, PACK * BANK], BF16, name="early", align_bytes=64)
         late = keep.tile([P, 2, PACK * BANK], BF16, name="late", align_bytes=64)
         early_q = (keep.tile([P, 2 * BANK], U32, name="early_codes", align_bytes=64),
                    keep.tile([P, 2 * BANK], U8, name="early_scales", align_bytes=64))
 
-        def quantise_early(lo, width):
+        def quantise_early(col, count):
             nc.vector.quantize_mx(
-                out=early_q[0][:, lo : lo + width].bitcast(FP8X4), scales=early_q[1][:, lo : lo + width],
-                in_=early[:].rearrange("p a c -> p (a c)")[:, PACK * lo : PACK * (lo + width)])
+                out=early_q[0][:, col : col + count].bitcast(FP8X4), scales=early_q[1][:, col : col + count],
+                in_=early[:].rearrange("p a c -> p (a c)")[:, PACK * col : PACK * (col + count)])
 
-        group_tf(0)
+        weave_tf(0)
         quantise_early(0, HALF)
-        group_wt_first(0)
-        group_wt_first(1)
+        for i in range(2):
+            weave_wt(nc.vector.tensor_copy, early[:, 1, :], wt_first[i], P // 2 * i, P // 2 * (i + 1), P // 2 * i)
         wr_w = wr_w + deal_words(wr_rest, 1, "wr_wp2")
-        quantise_early(BANK, BANK)
-        planes = [project(0, by_half)]
-        group_tf(1)
+        quantise_early(M, BANK)
+
+        planes = [project(0, [(t, part) for part in range(2) for t in range(PACK)])]
+        by_plane = [(t, part) for t in range(PACK) for part in range(2)]
+        weave_tf(1)
         planes.append(project(1, by_plane))
-        group_wt(1, late[:, 0, :], nc.scalar.copy, 0, SHARE)
+        weave_wt(nc.scalar.copy, late[:, 0, :], wt_raw[1], 0, SCALAR_SHARE, 0)
         planes.append(project(2, by_plane))
 
         x = [pick(0, planes[0])]
         quantise_early(HALF, HALF)
-        group_wt(1, late[:, 0, :], nc.vector.tensor_copy, SHARE, P)
-        group_wt(2, late[:, 1, :], nc.vector.tensor_copy)
+        weave_wt(nc.vector.tensor_copy, late[:, 0, :], wt_raw[1], SCALAR_SHARE, P, 0)
+        weave_wt(nc.vector.tensor_copy, late[:, 1, :], wt_raw[2], 0, P, 0)
         x.append(pick(1, planes[1]))
         late_q = quantise(late[:].rearrange("p a c -> p (a c)"), 2 * BANK, "late")
         x.append(pick(2, planes[2]))
-        wt_q = [early_q + (BANK,), late_q + (0,), late_q + (BANK,)]
-        nc.scalar.mul(halves[:], ends[:, :, 0 : N // P], 0.5)
+        wt_q = [early_q + (M,), late_q + (0,), late_q + (BANK,)]
+        nc.scalar.mul(halved[:], ends[:, :, 0:TYPE_TILES], 0.5)
 
-        def magnitudes(b, lo, width, offset, first_bank):
-            codes, scales, first = wt_q[b]
-            size = loads.tile([P, PACK, width], F32, name="size%d_%d" % (b, lo), offset=offset)
-            side = BANK // width
-            for k in range(PACK // side):
-                acc = psum.tile([P, side, width], F32, name="angle", tag="bank%d" % (first_bank + k))
-                for t in range(side * k, side * (k + 1)):
-                    cols = slice(first + P * t, first + P * (t + 1))
+        def magnitudes(b, lo, width, first_bank):
+            codes, scales, col = wt_q[b]
+            size = staged.tile([P, PACK, width], F32, name="size%d_%d" % (b, lo), offset=AT_SIZE[b, lo])
+            per_bank = BANK // width
+            for k in range(PACK // per_bank):
+                acc = psum.tile([P, per_bank, width], F32, name="angle", tag="bank%d" % (first_bank + k))
+                for t in range(per_bank * k, per_bank * (k + 1)):
+                    cols = slice(col + P * t, col + P * (t + 1))
                     nc.tensor.matmul_mx(
-                        out=acc[:, t % side, :], lhsT=codes[:, cols].bitcast(FP8X4), lhsT_scale=scales[:, cols],
+                        out=acc[:, t % per_bank, :], lhsT=codes[:, cols].bitcast(FP8X4), lhsT_scale=scales[:, cols],
                         rhs=early_q[0][:, lo : lo + width].bitcast(FP8X4), rhs_scale=early_q[1][:, lo : lo + width],
                         start=True, stop=True)
-                for t in range(side * k, side * (k + 1)):
-                    nc.scalar.activation(out=size[:, t, :], in_=acc[:, t % side, :], func=ACT.Abs, bias=phase_sb[:, b, t : t + 1])
+                for t in range(per_bank * k, per_bank * (k + 1)):
+                    nc.scalar.activation(out=size[:, t, :], in_=acc[:, t % per_bank, :], func=ACT.Abs,
+                                         bias=phase_sb[:, b, t : t + 1])
             return size
 
         def cosine(b, size, lo, width):
-            cos = keep.tile([P, PACK, width], F32, name="cos%d_%d" % (b, lo))
-            nc.scalar.activation(out=cos[:], in_=size, func=ACT.Sin, bias=half_pi[:], scale=-1.0)
-            return cos
+            values = keep.tile([P, PACK, width], F32, name="cos%d_%d" % (b, lo))
+            nc.scalar.activation(out=values[:], in_=size, func=ACT.Sin, bias=half_pi[:], scale=-1.0)
+            return values
 
-        AT = {(0, 0): 0, (1, 0): 24576, (2, 0): 28672, (1, HALF): 32768, (2, HALF): 36864}
-        size0 = magnitudes(0, 0, M, AT[0, 0], 0)
-        cos = {(0, 0): cosine(0, size0[:, :, 0:HALF], 0, HALF)}
-        for b in range(1, BLOCKS):
-            cos[b, 0] = cosine(b, magnitudes(b, 0, HALF, AT[b, 0], 2 + 2 * b)[:], 0, HALF)
-        cos[0, HALF] = cosine(0, size0[:, :, HALF:M], HALF, HALF)
-        cos[1, HALF] = cosine(1, magnitudes(1, HALF, HALF, AT[1, HALF], 0)[:], HALF, HALF)
-        last = magnitudes(2, HALF, HALF, AT[2, HALF], 2)
-        cos[2, HALF] = cosine(2, last[:, :, 0:QUARTER], HALF, QUARTER)
-        cos[2, HALF + QUARTER] = cosine(2, last[:, :, QUARTER:HALF], HALF + QUARTER, QUARTER)
+        size_first = magnitudes(0, 0, M, 0)
+        cos = {(0, 0): cosine(0, size_first[:, :, 0:HALF], 0, HALF)}
+        cos[1, 0] = cosine(1, magnitudes(1, 0, HALF, 4)[:], 0, HALF)
+        cos[2, 0] = cosine(2, magnitudes(2, 0, HALF, 6)[:], 0, HALF)
+        cos[0, HALF] = cosine(0, size_first[:, :, HALF:M], HALF, HALF)
+        cos[1, HALF] = cosine(1, magnitudes(1, HALF, HALF, 0)[:], HALF, HALF)
+        size_last = magnitudes(2, HALF, HALF, 2)
+        cos[2, HALF] = cosine(2, size_last[:, :, 0:QUARTER], HALF, QUARTER)
+        cos[2, HALF + QUARTER] = cosine(2, size_last[:, :, QUARTER:HALF], HALF + QUARTER, QUARTER)
 
-        steps = [(0, 0, HALF), (1, 0, HALF), (2, 0, HALF), (0, HALF, HALF), (1, HALF, HALF),
-                 (2, HALF, QUARTER), (2, HALF + QUARTER, QUARTER)]
-        homes = [AT[1, 0], AT[2, 0], AT[0, 0], AT[1, HALF], None, AT[2, HALF], None]
+        steps = [(b, 0, HALF) for b in range(GROUPS)] + [(b, HALF, HALF) for b in range(LAST)]
+        steps = steps + [(LAST, lo, width) for lo, width in PIECES[1:]]
+        freed_by = {(1, 0): AT_SIZE[1, 0], (2, 0): AT_SIZE[2, 0], (0, HALF): AT_SIZE[0, 0],
+                    (1, HALF): AT_SIZE[1, HALF], (2, HALF + QUARTER): AT_SIZE[2, HALF]}
         z_q = {}
-        z = [modulate(0, cos[0, 0][:], 0, HALF)]
+        z_woven = [modulate(*steps[0])]
         for i, (b, lo, width) in enumerate(steps):
+            home = None
             if i + 1 < len(steps):
-                nb, nlo, nwidth = steps[i + 1]
-                z.append(modulate(nb, cos[nb, nlo][:], nlo, nwidth))
-            z_q[b, lo] = quantise(z[i][:], width, "z%d_%d" % (b, lo), homes[i])
+                z_woven.append(modulate(*steps[i + 1]))
+                home = freed_by.get(steps[i + 1][0:2])
+            z_q[b, lo] = quantise(z_woven[i][:], width, "z%d_%d" % (b, lo), home)
 
-        types = N // P
         out_v = out.rearrange("(u p) m -> p u m", p=P)
 
-        def forecast(piece, banks):
-            lo, width = PIECES[piece]
+        for piece, (lo, width) in enumerate(PIECES):
             sums, opens, closes = [], [], []
-            for bank, count in banks:
+            for bank, count in SUM_BANKS[piece]:
                 acc = psum.tile([P, count, width], F32, name="y%d_%d" % (piece, bank), tag="bank%d" % bank)
                 sums.extend(acc[:, i, :] for i in range(count))
                 opens.extend(i == 0 for i in range(count))
                 closes.extend(i == count - 1 for i in range(count))
-            for b in range(BLOCKS):
-                start = lo if (b, lo) in z_q else HALF
-                codes, scales = z_q[b, start]
-                within = slice(lo - start, lo - start + width)
-                for u in range(types):
+            for b in range(GROUPS):
+                z_lo = lo if (b, lo) in z_q else HALF
+                codes, scales = z_q[b, z_lo]
+                within = slice(lo - z_lo, lo - z_lo + width)
+                for u in range(TYPE_TILES):
                     nc.tensor.matmul_mx(
                         out=sums[u], lhsT=wf_w[:, b, P * u : P * (u + 1)].bitcast(FP8X4),
                         lhsT_scale=wf_s[:, b, P * u : P * (u + 1)],
                         rhs=codes[:, within].bitcast(FP8X4), rhs_scale=scales[:, within],
-                        start=(b == 0 and opens[u]), stop=(b == BLOCKS - 1 and closes[u]))
+                        start=(b == 0 and opens[u]), stop=(b == LAST and closes[u]))
             if piece == 0:
-                tanh = loads.tile([P, types, width], F32, name="tanh0", offset=AT[2, HALF] + 2 * HALF)
+                tanh = staged.tile([P, TYPE_TILES, width], F32, name="tanh0", offset=AT_SIZE[2, HALF] + 4 * QUARTER)
             else:
-                tanh = keep.tile([P, types, width], F32, name="tanh%d" % piece)
-            for first, group in STORES[piece]:
-                res = keep.tile([P, group, width], F32, name="res%d_%d" % (piece, first))
-                for u in range(first, first + group):
+                tanh = keep.tile([P, TYPE_TILES, width], F32, name="tanh%d" % piece)
+            for u_first, tiles in STORES[piece]:
+                res = keep.tile([P, tiles, width], F32, name="res%d_%d" % (piece, u_first))
+                for u in range(u_first, u_first + tiles):
                     nc.scalar.activation(out=tanh[:, u, :], in_=sums[u], func=ACT.Tanh,
                                          bias=half_bf[:, u : u + 1], scale=0.5)
-                    nc.vector.tensor_scalar(res[:, u - first, :], tanh[:, u, :], half_sev[:, u : u + 1], half_sev[:, u : u + 1], ALU.mult, ALU.add)
-                nc.sync.dma_start(out_v[:, first : first + group, lo : lo + width], res[:])
-
-        forecast(0, [(4, 2), (5, 2)])
-        forecast(1, [(0, 1), (1, 1), (6, 2)])
-        forecast(2, [(2, 1), (3, 1), (7, 2)])
+                    nc.vector.tensor_scalar(res[:, u - u_first, :], tanh[:, u, :], half_sev[:, u : u + 1],
+                                            half_sev[:, u : u + 1], ALU.mult, ALU.add)
+                nc.sync.dma_start(out_v[:, u_first : u_first + tiles, lo : lo + width], res[:])

@@ -26,7 +26,7 @@ TYPE_TILES = N // P
 HALF = M // 2
 QUARTER = M // 4
 
-SCALAR_SHARE = 64
+SCALAR_SHARE = 32
 
 PIECES = [(0, HALF), (HALF, QUARTER), (HALF + QUARTER, QUARTER)]
 STORES = [[(0, 1), (1, 1), (2, 1), (3, 1)], [(0, 4)], [(0, 2), (2, 1), (3, 1)]]
@@ -126,9 +126,9 @@ def tile_list_event_graph_forecast_kernel(
 
         def deal_scales(b, groups):
             scales = keep.tile([P, groups * BANK], U8, name="wr_sp%d" % b, align_bytes=64)
-            nc.vector.tensor_copy(
-                scales[:].rearrange("p (b t c) -> p b c t", b=groups, t=PACK),
-                wr_s[:, BANK * b : BANK * (b + groups)].rearrange("p (b c t) -> p b c t", b=groups, t=PACK))
+            nc.gpsimd.tensor_copy(
+                scales[:].rearrange("p (b t c) -> p b t c", b=groups, t=PACK),
+                wr_s[:, BANK * b : BANK * (b + groups)].rearrange("p (b c t) -> p b t c", b=groups, t=PACK))
             return [scales[:, BANK * i : BANK * (i + 1)] for i in range(groups)]
 
         def gather_words(part, offset):
@@ -189,7 +189,7 @@ def tile_list_event_graph_forecast_kernel(
         nc.vector.tensor_copy(v_s[:], tab_s[:].indirect(idx[:]))
         v_w = [gather_words(0, AT_V_W)]
         wr_p = deal_scales(0, 1) + deal_scales(1, LAST)
-        v_w.append(gather_words(1, AT_WR_S))
+        v_w.append(gather_words(1, AT_V_W + 2 * KIB))
 
         early = keep.tile([P, 2, PACK * BANK], BF16, name="early", align_bytes=64)
         late = keep.tile([P, 2, PACK * BANK], BF16, name="late", align_bytes=64)

@@ -26,7 +26,7 @@ TYPE_TILES = N // P
 HALF = M // 2
 QUARTER = M // 4
 
-SCALAR_SHARE = 32
+SCALAR_SHARE = 96
 
 PIECES = [(0, HALF), (HALF, QUARTER), (HALF + QUARTER, QUARTER)]
 STORES = [[(0, 1), (1, 1), (2, 1), (3, 1)], [(0, 4)], [(0, 2), (2, 1), (3, 1)]]
@@ -78,9 +78,7 @@ def tile_list_event_graph_forecast_kernel(
         tf_raw = [staged.tile([P, PACK, S], F32, name="tf_raw0", offset=AT_TF_FIRST)[:, :, 0:HALF],
                   staged.tile([P, PACK, HALF], F32, name="tf_raw1", offset=AT_TF_SECOND)[:]]
         wt_raw = {b: staged.tile([P, PACK, BANK], F32, name="wt_raw%d" % b, offset=AT_WT + 8 * KIB * b)
-                  for b in range(1, GROUPS)}
-        wt_first = [staged.tile([P, PACK, BANK // 2], F32, name="wt_first%d" % i, offset=AT_WT + 4 * KIB * i)
-                    for i in range(2)]
+                  for b in range(GROUPS)}
 
         nc.gpsimd.memset(tab_s[:].bitcast(I32), 0)
         nc.vector.memset(wr_s[:].bitcast(I32), 0)
@@ -103,11 +101,10 @@ def tile_list_event_graph_forecast_kernel(
         nc.sync.dma_start(tab_w[:].bitcast(I32), tab_words[0].rearrange("p t i -> p (t i)").bitcast(I32))
         load_scale_rows(wr_s, wr_scales[0])
         load_k_rows(tf_raw[0], tf, 0, HALF)
-        for i in range(2):
-            load_k_rows(wt_first[i][:], wt, BANK // 2 * i, BANK // 2)
+        load_k_rows(tf_raw[1], tf, HALF, HALF)
         nc.sync.dma_start(wr_rest[:].bitcast(I32), wr_words[0, :, 2 * BANK * LAST :].bitcast(I32))
         nc.sync.dma_start(wgt_sb[:], wgt)
-        load_k_rows(tf_raw[1], tf, HALF, HALF)
+        load_k_rows(wt_raw[0][:], wt, 0, BANK)
         nc.sync.dma_start(phase_sb[:], phase.rearrange("(b p i) -> p b i", b=GROUPS, i=PACK))
         for b in range(1, GROUPS):
             load_k_rows(wt_raw[b][:], wt, BANK * b, BANK)
@@ -145,9 +142,9 @@ def tile_list_event_graph_forecast_kernel(
             nc.vector.quantize_mx(out=codes[:].bitcast(FP8X4), scales=scales[:], in_=woven)
             return codes, scales
 
-        def weave_tf(i):
-            nc.scalar.copy(
-                early[:, 0, PACK * HALF * i : PACK * HALF * (i + 1)].rearrange("p (c e j) -> p c j e", j=PACK, e=4),
+        def weave_tf(copy, i):
+            copy(
+                tf_woven[:, PACK * HALF * i : PACK * HALF * (i + 1)].rearrange("p (c e j) -> p c j e", j=PACK, e=4),
                 tf_raw[i].rearrange("p j (c e) -> p c j e", e=4))
 
         def weave_wt(copy, woven, raw, c_from, c_to, c_raw):
@@ -167,13 +164,15 @@ def tile_list_event_graph_forecast_kernel(
                 nc.scalar.copy(planes[t][:, BANK * part : BANK * (part + 1)], acc[:])
             return planes
 
-        def pick(b, planes):
+        def pick(b, planes, between=None):
             if b == LAST:
                 picked = staged.tile([P, PACK, M], F32, name="x_last", offset=AT_WT + 8 * KIB * LAST)
             else:
                 picked = keep.tile([P, PACK, M], F32, name="x%d" % b)
             for t in range(PACK):
                 nc.vector.tensor_tensor(picked[:, t, :], planes[t][:].indirect(idx2[:]), wgt_sb[:], ALU.mult)
+                if between and t in between:
+                    between[t]()
             return picked
 
         def modulate(b, lo, width):
@@ -187,42 +186,39 @@ def tile_list_event_graph_forecast_kernel(
         wr_w = deal_words(wr_first, LAST, "wr_wp0")
         v_s = keep.tile([P, S], U8, name="v_s", align_bytes=64)
         nc.vector.tensor_copy(v_s[:], tab_s[:].indirect(idx[:]))
+        for i in range(3):
+            idle = psum.tile([P, BANK], F32, name="idle", tag="bank%d" % (7 - i))
+            nc.tensor.matmul_mx(
+                out=idle[:], lhsT=wr_w[0][:, 0 : 2 * P].bitcast(FP4X4), lhsT_scale=tab_s[:, 0:P],
+                rhs=tab_w[:, 0:BANK].bitcast(FP8X4), rhs_scale=tab_s[:, 0:BANK], start=True, stop=True)
         v_w = [gather_words(0, AT_V_W)]
         wr_p = deal_scales(0, 1) + deal_scales(1, LAST)
         v_w.append(gather_words(1, AT_V_W + 2 * KIB))
 
-        early = keep.tile([P, 2, PACK * BANK], BF16, name="early", align_bytes=64)
+        tf_woven = keep.tile([P, PACK * M], BF16, name="tf_woven", align_bytes=64)
         late = keep.tile([P, 2, PACK * BANK], BF16, name="late", align_bytes=64)
-        early_q = (keep.tile([P, 2 * BANK], U32, name="early_codes", align_bytes=64),
-                   keep.tile([P, 2 * BANK], U8, name="early_scales", align_bytes=64))
 
-        def quantise_early(col, count):
-            nc.vector.quantize_mx(
-                out=early_q[0][:, col : col + count].bitcast(FP8X4), scales=early_q[1][:, col : col + count],
-                in_=early[:].rearrange("p a c -> p (a c)")[:, PACK * col : PACK * (col + count)])
-
-        weave_tf(0)
-        quantise_early(0, HALF)
-        for i in range(2):
-            weave_wt(nc.vector.tensor_copy, early[:, 1, :], wt_first[i], P // 2 * i, P // 2 * (i + 1), P // 2 * i)
+        weave_tf(nc.scalar.copy, 0)
+        weave_tf(nc.vector.tensor_copy, 1)
         wr_w = wr_w + deal_words(wr_rest, 1, "wr_wp2")
-        quantise_early(M, BANK)
+        tf_q = quantise(tf_woven[:], M, "tf")
 
-        planes = [project(0, [(t, part) for part in range(2) for t in range(PACK)])]
         by_plane = [(t, part) for t in range(PACK) for part in range(2)]
-        weave_tf(1)
-        planes.append(project(1, by_plane))
+        planes = [project(0, by_plane), project(1, by_plane)]
         weave_wt(nc.scalar.copy, late[:, 0, :], wt_raw[1], 0, SCALAR_SHARE, 0)
         planes.append(project(2, by_plane))
 
-        x = [pick(0, planes[0])]
-        quantise_early(HALF, HALF)
+        wt0_woven = staged.tile([P, PACK * BANK], BF16, name="wt0_woven", align_bytes=64, offset=AT_TF_FIRST + 4 * S)
+        wt_q = []
+        x = [pick(0, planes[0], {
+            1: lambda: weave_wt(nc.vector.tensor_copy, wt0_woven[:], wt_raw[0], 0, P, 0),
+            2: lambda: wt_q.append(quantise(wt0_woven[:], BANK, "wt0", AT_TF_FIRST + 8 * S) + (0,))})]
         weave_wt(nc.vector.tensor_copy, late[:, 0, :], wt_raw[1], SCALAR_SHARE, P, 0)
         weave_wt(nc.vector.tensor_copy, late[:, 1, :], wt_raw[2], 0, P, 0)
         x.append(pick(1, planes[1]))
         late_q = quantise(late[:].rearrange("p a c -> p (a c)"), 2 * BANK, "late")
         x.append(pick(2, planes[2]))
-        wt_q = [early_q + (M,), late_q + (0,), late_q + (BANK,)]
+        wt_q = wt_q + [late_q + (0,), late_q + (BANK,)]
         nc.scalar.mul(halved[:], ends[:, :, 0:TYPE_TILES], 0.5)
 
         def magnitudes(b, lo, width, first_bank):
@@ -235,7 +231,7 @@ def tile_list_event_graph_forecast_kernel(
                     cols = slice(col + P * t, col + P * (t + 1))
                     nc.tensor.matmul_mx(
                         out=acc[:, t % per_bank, :], lhsT=codes[:, cols].bitcast(FP8X4), lhsT_scale=scales[:, cols],
-                        rhs=early_q[0][:, lo : lo + width].bitcast(FP8X4), rhs_scale=early_q[1][:, lo : lo + width],
+                        rhs=tf_q[0][:, lo : lo + width].bitcast(FP8X4), rhs_scale=tf_q[1][:, lo : lo + width],
                         start=True, stop=True)
                 for t in range(per_bank * k, per_bank * (k + 1)):
                     nc.scalar.activation(out=size[:, t, :], in_=acc[:, t % per_bank, :], func=ACT.Abs,

@@ -88,8 +88,8 @@ def tile_list_event_graph_forecast_kernel(
         nc.gpsimd.memset(wf_s[:].rearrange("p a c -> p (a c)").bitcast(I32), 0)
 
         def load_scale_rows(scale_tile, rows):
-            for q in range(4):
-                nc.sync.dma_start(scale_tile[32 * q : 32 * q + 4].bitcast(I32), rows[4 * q : 4 * q + 4].bitcast(I32))
+            for r in range(4):
+                nc.sync.dma_start(scale_tile[r : P : 32].bitcast(I32), rows[r : 16 : 4].bitcast(I32))
 
         def load_k_rows(raw, source, col, count):
             nc.sync.dma_start(raw, source[:, col : col + count].rearrange("(p j) c -> p j c", j=PACK))

@@ -45,6 +45,7 @@ AT_WT = 32 * KIB
 AT_TF_FIRST = 56 * KIB
 AT_WR_S = 72 * KIB
 AT_V_W = 74 * KIB
+AT_WR_DEALT = [78 * KIB, 82 * KIB]
 AT_SIZE = {(0, 0): AT_TAB_W, (1, 0): AT_TF_SECOND, (2, 0): AT_SPARE, (1, HALF): AT_WT, (2, HALF): AT_WT + 4 * KIB}
 
 
@@ -114,8 +115,8 @@ def tile_list_event_graph_forecast_kernel(
             nc.sync.dma_start(ends[:, 0, 0:TYPE_TILES], bf.rearrange("(u p) -> p u", p=P))
             nc.sync.dma_start(ends[:, 1, 0:TYPE_TILES], sev.rearrange("(u p) -> p u", p=P))
 
-        def deal_words(raw, groups, name):
-            words = keep.tile([P, groups * 2 * BANK], U8, name=name, align_bytes=64)
+        def deal_words(raw, groups, name, home):
+            words = staged.tile([P, groups * 2 * BANK], U8, name=name, align_bytes=64, offset=home)
             nc.vector.tensor_copy(
                 words[:].bitcast(U16).rearrange("p (b t c) -> p b c t", b=groups, t=PACK),
                 raw[:].bitcast(U16).rearrange("p (b c t) -> p b c t", b=groups, t=PACK))
@@ -147,9 +148,9 @@ def tile_list_event_graph_forecast_kernel(
                 tf_woven[:, PACK * HALF * i : PACK * HALF * (i + 1)].rearrange("p (c e j) -> p c j e", j=PACK, e=4),
                 tf_raw[i].rearrange("p j (c e) -> p c j e", e=4))
 
-        def weave_wt(copy, woven, raw, c_from, c_to, c_raw):
-            copy(woven.rearrange("p (t c j) -> p c j t", t=PACK, j=PACK)[:, c_from:c_to],
-                 raw[:].rearrange("p j (c t) -> p c j t", t=PACK)[:, c_from - c_raw : c_to - c_raw])
+        def weave_wt(copy, woven, b, t_from, t_to):
+            copy(woven.rearrange("p (t c j) -> p c j t", t=t_to - t_from, j=PACK),
+                 wt_raw[b][:].rearrange("p j (c t) -> p c j t", t=PACK)[:, :, :, t_from:t_to])
 
         def project(b, order):
             planes = [staged.tile([P, S], F32, name="h0_%d" % t, offset=AT_TF_FIRST + 4 * S * t) if b == 0
@@ -165,10 +166,7 @@ def tile_list_event_graph_forecast_kernel(
             return planes
 
         def pick(b, planes, between=None):
-            if b == LAST:
-                picked = staged.tile([P, PACK, M], F32, name="x_last", offset=AT_WT + 8 * KIB * LAST)
-            else:
-                picked = keep.tile([P, PACK, M], F32, name="x%d" % b)
+            picked = keep.tile([P, PACK, M], F32, name="x%d" % b)
             for t in range(PACK):
                 nc.vector.tensor_tensor(picked[:, t, :], planes[t][:].indirect(idx2[:]), wgt_sb[:], ALU.mult)
                 if between and t in between:
@@ -183,7 +181,7 @@ def tile_list_event_graph_forecast_kernel(
                 cos[b, lo][:].rearrange("p t (c e) -> p c t e", e=2), ALU.mult)
             return z
 
-        wr_w = deal_words(wr_first, LAST, "wr_wp0")
+        wr_w = deal_words(wr_first, LAST, "wr_wp0", AT_WR_DEALT[0])
         v_s = keep.tile([P, S], U8, name="v_s", align_bytes=64)
         nc.vector.tensor_copy(v_s[:], tab_s[:].indirect(idx[:]))
         for i in range(3):
@@ -196,39 +194,53 @@ def tile_list_event_graph_forecast_kernel(
         v_w.append(gather_words(1, AT_V_W + 2 * KIB))
 
         tf_woven = keep.tile([P, PACK * M], BF16, name="tf_woven", align_bytes=64)
-        late = keep.tile([P, 2, PACK * BANK], BF16, name="late", align_bytes=64)
 
         weave_tf(nc.scalar.copy, 0)
         weave_tf(nc.vector.tensor_copy, 1)
-        wr_w = wr_w + deal_words(wr_rest, 1, "wr_wp2")
+        wr_w = wr_w + deal_words(wr_rest, 1, "wr_wp2", AT_WR_DEALT[1])
         tf_q = quantise(tf_woven[:], M, "tf")
 
         by_plane = [(t, part) for t in range(PACK) for part in range(2)]
         planes = [project(0, by_plane), project(1, by_plane)]
-        weave_wt(nc.scalar.copy, late[:, 0, :], wt_raw[1], 0, SCALAR_SHARE, 0)
+        def woven_tile(name, count, home):
+            if home is None:
+                return keep.tile([P, PACK * P * count], BF16, name=name, align_bytes=64)
+            return staged.tile([P, PACK * P * count], BF16, name=name, align_bytes=64, offset=home)
+
+        wt0 = woven_tile("wt0", PACK, AT_WR_DEALT[0])
+        wt1_low = woven_tile("wt1_low", 2, None)
+        wt1_high = woven_tile("wt1_high", 2, AT_V_W + 2 * KIB)
+        wt2 = woven_tile("wt2", PACK, AT_WR_DEALT[1])
+        weave_wt(nc.scalar.copy, wt1_low[:], 1, 0, 2)
         planes.append(project(2, by_plane))
 
-        wt0_woven = staged.tile([P, PACK * BANK], BF16, name="wt0_woven", align_bytes=64, offset=AT_TF_FIRST + 4 * S)
-        wt_q = []
-        x = [pick(0, planes[0], {
-            1: lambda: weave_wt(nc.vector.tensor_copy, wt0_woven[:], wt_raw[0], 0, P, 0),
-            2: lambda: wt_q.append(quantise(wt0_woven[:], BANK, "wt0", AT_TF_FIRST + 8 * S) + (0,))})]
-        weave_wt(nc.vector.tensor_copy, late[:, 0, :], wt_raw[1], SCALAR_SHARE, P, 0)
-        weave_wt(nc.vector.tensor_copy, late[:, 1, :], wt_raw[2], 0, P, 0)
+        wt_q = {}
+
+        def quantise_wt(woven, b, t_from, t_to, home):
+            codes, scales = quantise(woven[:], P * (t_to - t_from), "wt%d_%d" % (b, t_from), home)
+            for t in range(t_from, t_to):
+                wt_q.setdefault((b, t), (codes, scales, P * (t - t_from)))
+
+        x = [pick(0, planes[0])]
+        weave_wt(nc.vector.tensor_copy, wt0[:], 0, 0, PACK)
         x.append(pick(1, planes[1]))
-        late_q = quantise(late[:].rearrange("p a c -> p (a c)"), 2 * BANK, "late")
+        quantise_wt(wt0, 0, 0, PACK, AT_V_W)
+        weave_wt(nc.vector.tensor_copy, wt1_high[:], 1, 2, PACK)
+        weave_wt(nc.vector.tensor_copy, wt2[:], 2, 0, PACK)
+        quantise_wt(wt1_low, 1, 0, 2, None)
+        quantise_wt(wt1_high, 1, 2, PACK, None)
+        quantise_wt(wt2, 2, 0, PACK, None)
         x.append(pick(2, planes[2]))
-        wt_q = wt_q + [late_q + (0,), late_q + (BANK,)]
         nc.scalar.mul(halved[:], ends[:, :, 0:TYPE_TILES], 0.5)
 
         def magnitudes(b, lo, width, first_bank):
-            codes, scales, col = wt_q[b]
             size = staged.tile([P, PACK, width], F32, name="size%d_%d" % (b, lo), offset=AT_SIZE[b, lo])
             per_bank = BANK // width
             for k in range(PACK // per_bank):
                 acc = psum.tile([P, per_bank, width], F32, name="angle", tag="bank%d" % (first_bank + k))
                 for t in range(per_bank * k, per_bank * (k + 1)):
-                    cols = slice(col + P * t, col + P * (t + 1))
+                    codes, scales, col = wt_q[b, t]
+                    cols = slice(col, col + P)
                     nc.tensor.matmul_mx(
                         out=acc[:, t % per_bank, :], lhsT=codes[:, cols].bitcast(FP8X4), lhsT_scale=scales[:, cols],
                         rhs=tf_q[0][:, lo : lo + width].bitcast(FP8X4), rhs_scale=tf_q[1][:, lo : lo + width],

@@ -184,11 +184,6 @@ def tile_list_event_graph_forecast_kernel(
         wr_w = deal_words(wr_first, LAST, "wr_wp0", AT_WR_DEALT[0])
         v_s = keep.tile([P, S], U8, name="v_s", align_bytes=64)
         nc.vector.tensor_copy(v_s[:], tab_s[:].indirect(idx[:]))
-        for i in range(3):
-            idle = psum.tile([P, BANK], F32, name="idle", tag="bank%d" % (7 - i))
-            nc.tensor.matmul_mx(
-                out=idle[:], lhsT=wr_w[0][:, 0 : 2 * P].bitcast(FP4X4), lhsT_scale=tab_s[:, 0:P],
-                rhs=tab_w[:, 0:BANK].bitcast(FP8X4), rhs_scale=tab_s[:, 0:BANK], start=True, stop=True)
         v_w = [gather_words(0, AT_V_W)]
         wr_p = deal_scales(0, 1) + deal_scales(1, LAST)
         v_w.append(gather_words(1, AT_V_W + 2 * KIB))

import math
from contextlib import ExitStack

import concourse.mybir as mybir

T, S, M, H, N = 2048, 1024, 512, 1536, 512
FLOPS = 2 * 512 * H * S + 2 * 512 * H * M + 2 * H * N * M

F32 = mybir.dt.float32
BF16 = mybir.dt.bfloat16
I32 = mybir.dt.int32
U32 = mybir.dt.uint32
U16 = mybir.dt.uint16
U8 = mybir.dt.uint8
FP8X4 = mybir.dt.float8_e4m3fn_x4
FP4X4 = mybir.dt.float4_e2m1fn_x4
ACT = mybir.ActivationFunctionType
ALU = mybir.AluOpType

P = 128
PACK = 4
GROUPS = H // (P * PACK)
LAST = GROUPS - 1
BANK = 512
TYPE_TILES = N // P
HALF = M // 2
QUARTER = M // 4

SCALAR_SHARE = 96

PIECES = [(0, HALF), (HALF, QUARTER), (HALF + QUARTER, QUARTER)]
STORES = [[(0, 1), (1, 1), (2, 1), (3, 1)], [(0, 4)], [(0, 2), (2, 1), (3, 1)]]
SUM_BANKS = [[(4, 2), (5, 2)], [(0, 1), (1, 1), (6, 2)], [(2, 1), (3, 1), (7, 2)]]

KIB = 1024
AT_TAB_W = 0
AT_WR_REST = 9 * KIB
AT_WF_W = 12 * KIB
AT_WGT = 18 * KIB
AT_PHASE = 20 * KIB
AT_ENDS = AT_PHASE + 64
AT_TF_SECOND = 24 * KIB
AT_SPARE = 28 * KIB
AT_WT = 32 * KIB
AT_TF_FIRST = 56 * KIB
AT_WR_S = 72 * KIB
AT_V_W = 74 * KIB
AT_WR_DEALT = [78 * KIB, 82 * KIB]
AT_SIZE = {(0, 0): AT_TAB_W, (1, 0): AT_TF_SECOND, (2, 0): AT_SPARE, (1, HALF): AT_WT, (2, HALF): AT_WT + 4 * KIB}


def tile_list_event_graph_forecast_kernel(
    tc, tab_words, tab_scales, offs, wr_words, wr_scales, offs2, wgt, tf, wt, phase,
    wf_words, wf_scales, bf, sev, out,
):
    nc = tc.nc
    with ExitStack() as ctx:
        keep = ctx.enter_context(tc.tile_pool(name="keep", bufs=1))
        staged = ctx.enter_context(tc.tile_pool(name="loads", bufs=1))
        psum = ctx.enter_context(tc.psum_pool(name="psum", bufs=1))

        idx = keep.tile([P, S // 16], U16, name="idx")
        idx2 = keep.tile([P, M // 16], U16, name="idx2")
        tab_s = keep.tile([P, T], U8, name="tab_s", align_bytes=64)
        wr_s = staged.tile([P, H], U8, name="wr_s", align_bytes=64, offset=AT_WR_S)
        wf_s = keep.tile([P, GROUPS, N], U8, name="wf_s", align_bytes=64)
        halved = keep.tile([P, 2, TYPE_TILES], F32, name="halves")
        half_bf, half_sev = halved[:, 0, :], halved[:, 1, :]
        half_pi = keep.tile([P, 1], F32, name="half_pi")
        warm = keep.tile([P, 1], F32, name="warm")
        one = staged.tile([P, AT_WR_S // 4], F32, name="one", offset=0)
        tab_w = staged.tile([P, T], U32, name="tab_w", align_bytes=64, offset=AT_TAB_W)
        wr_first = keep.tile([P, 2 * BANK * LAST], U8, name="wr_first", align_bytes=64)
        wr_rest = staged.tile([P, 2 * BANK], U8, name="wr_rest", align_bytes=64, offset=AT_WR_REST)
        wf_w = staged.tile([P, GROUPS, N], U32, name="wf_w", align_bytes=64, offset=AT_WF_W)
        wgt_sb = staged.tile([P, M], F32, name="wgt_sb", offset=AT_WGT)
        phase_sb = staged.tile([P, GROUPS, PACK], F32, name="phase_sb", offset=AT_PHASE)
        ends = staged.tile([P, 2, 8], F32, name="ends", offset=AT_ENDS)
        tf_raw = [staged.tile([P, PACK, S], F32, name="tf_raw0", offset=AT_TF_FIRST)[:, :, 0:HALF],
                  staged.tile([P, PACK, HALF], F32, name="tf_raw1", offset=AT_TF_SECOND)[:]]
        wt_raw = {b: staged.tile([P, PACK, BANK], F32, name="wt_raw%d" % b, offset=AT_WT + 8 * KIB * b)
                  for b in range(GROUPS)}

        nc.gpsimd.memset(tab_s[:].bitcast(I32), 0)
        nc.vector.memset(wr_s[:].bitcast(I32), 0)
        nc.gpsimd.memset(one[:, 0:1], 1.0)
        nc.vector.tensor_scalar(half_pi[:], one[:, 0:1], 0.5 * math.pi, None, ALU.mult)
        nc.scalar.activation(out=warm[:], in_=half_pi[:], func=ACT.Silu)
        nc.gpsimd.memset(wf_s[:].rearrange("p a c -> p (a c)").bitcast(I32), 0)

        def load_scale_rows(scale_tile, rows):
            for r in range(4):
                nc.sync.dma_start(scale_tile[r : P : 32].bitcast(I32), rows[r : 16 : 4].bitcast(I32))

        def load_k_rows(raw, source, col, count):
            nc.sync.dma_start(raw, source[:, col : col + count].rearrange("(p j) c -> p j c", j=PACK))

        nc.sync.dma_start(wr_first[:].bitcast(I32), wr_words[0, :, 0 : 2 * BANK * LAST].bitcast(I32))
        nc.sync.dma_start(idx[:], offs)
        nc.sync.dma_start(idx2[:], offs2)
        load_scale_rows(tab_s, tab_scales[0])
        nc.sync.dma_start(tab_w[:].bitcast(I32), tab_words[0].rearrange("p t i -> p (t i)").bitcast(I32))
        load_scale_rows(wr_s, wr_scales[0])
        load_k_rows(tf_raw[0], tf, 0, HALF)
        load_k_rows(tf_raw[1], tf, HALF, HALF)
        nc.sync.dma_start(wr_rest[:].bitcast(I32), wr_words[0, :, 2 * BANK * LAST :].bitcast(I32))
        nc.sync.dma_start(wgt_sb[:], wgt)
        load_k_rows(wt_raw[0][:], wt, 0, BANK)
        nc.sync.dma_start(phase_sb[:], phase.rearrange("(b p i) -> p b i", b=GROUPS, i=PACK))
        for b in range(1, GROUPS):
            load_k_rows(wt_raw[b][:], wt, BANK * b, BANK)
        nc.sync.dma_start(wf_w[:].bitcast(I32), wf_words.rearrange("a p c i -> p a (c i)").bitcast(I32))
        load_scale_rows(wf_s, wf_scales.rearrange("a r c -> r a c"))
        with nc.allow_non_contiguous_dma(reason="one value a partition"):
            nc.sync.dma_start(ends[:, 0, 0:TYPE_TILES], bf.rearrange("(u p) -> p u", p=P))
            nc.sync.dma_start(ends[:, 1, 0:TYPE_TILES], sev.rearrange("(u p) -> p u", p=P))

        def deal_words(raw, groups, name, home):
            words = staged.tile([P, groups * 2 * BANK], U8, name=name, align_bytes=64, offset=home)
            nc.vector.tensor_copy(
                words[:].bitcast(U16).rearrange("p (b t c) -> p b c t", b=groups, t=PACK),
                raw[:].bitcast(U16).rearrange("p (b c t) -> p b c t", b=groups, t=PACK))
            return [words[:, 2 * BANK * i : 2 * BANK * (i + 1)] for i in range(groups)]

        def deal_scales(b, groups):
            scales = keep.tile([P, groups * BANK], U8, name="wr_sp%d" % b, align_bytes=64)
            nc.gpsimd.tensor_copy(
                scales[:].rearrange("p (b t c) -> p b t c", b=groups, t=PACK),
                wr_s[:, BANK * b : BANK * (b + groups)].rearrange("p (b c t) -> p b t c", b=groups, t=PACK))
            return [scales[:, BANK * i : BANK * (i + 1)] for i in range(groups)]

        def gather_words(part, offset):
            words = staged.tile([P, BANK], U32, name="v_w%d" % part, align_bytes=64, offset=offset)
            nc.vector.tensor_copy(words[:], tab_w[:].indirect(idx[:, BANK // 16 * part : BANK // 16 * (part + 1)]))
            return words

        def quantise(woven, columns, name, offset=None):
            if offset is None:
                codes = keep.tile([P, columns], U32, name=name + "_codes", align_bytes=64)
            else:
                codes = staged.tile([P, columns], U32, name=name + "_codes", align_bytes=64, offset=offset)
            scales = keep.tile([P, columns], U8, name=name + "_scales", align_bytes=64)
            nc.vector.quantize_mx(out=codes[:].bitcast(FP8X4), scales=scales[:], in_=woven)
            return codes, scales

        def weave_tf(copy, i):
            copy(
                tf_woven[:, PACK * HALF * i : PACK * HALF * (i + 1)].rearrange("p (c e j) -> p c j e", j=PACK, e=4),
                tf_raw[i].rearrange("p j (c e) -> p c j e", e=4))

        def weave_wt(copy, woven, b, t_from, t_to):
            copy(woven.rearrange("p (t c j) -> p c j t", t=t_to - t_from, j=PACK),
                 wt_raw[b][:].rearrange("p j (c t) -> p c j t", t=PACK)[:, :, :, t_from:t_to])

        def project(b, order):
            planes = [staged.tile([P, S], F32, name="h0_%d" % t, offset=AT_TF_FIRST + 4 * S * t) if b == 0
                      else keep.tile([P, S], F32, name="h%d_%d" % (b, t)) for t in range(PACK)]
            for bank, (t, part) in enumerate(order):
                acc = psum.tile([P, BANK], F32, name="h_acc", tag="bank%d" % bank)
                nc.tensor.matmul_mx(
                    out=acc[:], lhsT=wr_w[b][:, 2 * P * t : 2 * P * (t + 1)].bitcast(FP4X4),
                    lhsT_scale=wr_p[b][:, P * t : P * (t + 1)],
                    rhs=v_w[part][:].bitcast(FP8X4), rhs_scale=v_s[:, BANK * part : BANK * (part + 1)],
                    start=True, stop=True)
                nc.scalar.copy(planes[t][:, BANK * part : BANK * (part + 1)], acc[:])
            return planes

        def pick(b, planes, between=None):
            picked = keep.tile([P, PACK, M], F32, name="x%d" % b)
            for t in range(PACK):
                nc.vector.tensor_tensor(picked[:, t, :], planes[t][:].indirect(idx2[:]), wgt_sb[:], ALU.mult)
                if between and t in between:
                    between[t]()
            return picked

        def modulate(b, lo, width):
            z = keep.tile([P, PACK * width], BF16, name="z%d_%d" % (b, lo), align_bytes=64)
            nc.vector.tensor_tensor(
                z[:].rearrange("p (c e t) -> p c t e", t=PACK, e=2),
                x[b][:, :, lo : lo + width].rearrange("p t (c e) -> p c t e", e=2),
                cos[b, lo][:].rearrange("p t (c e) -> p c t e", e=2), ALU.mult)
            return z

        wr_w = deal_words(wr_first, LAST, "wr_wp0", AT_WR_DEALT[0])
        v_s = keep.tile([P, S], U8, name="v_s", align_bytes=64)
        nc.vector.tensor_copy(v_s[:], tab_s[:].indirect(idx[:]))
        v_w = [gather_words(0, AT_V_W)]
        wr_p = deal_scales(0, 1) + deal_scales(1, LAST)
        v_w.append(gather_words(1, AT_V_W + 2 * KIB))

        tf_woven = keep.tile([P, PACK * M], BF16, name="tf_woven", align_bytes=64)

        weave_tf(nc.scalar.copy, 0)
        weave_tf(nc.vector.tensor_copy, 1)
        wr_w = wr_w + deal_words(wr_rest, 1, "wr_wp2", AT_WR_DEALT[1])
        tf_q = quantise(tf_woven[:], M, "tf")

        by_plane = [(t, part) for t in range(PACK) for part in range(2)]
        planes = [project(0, by_plane), project(1, by_plane)]
        def woven_tile(name, count, home):
            if home is None:
                return keep.tile([P, PACK * P * count], BF16, name=name, align_bytes=64)
            return staged.tile([P, PACK * P * count], BF16, name=name, align_bytes=64, offset=home)

        wt0 = woven_tile("wt0", PACK, AT_WR_DEALT[0])
        wt1_low = woven_tile("wt1_low", 2, None)
        wt1_high = woven_tile("wt1_high", 2, AT_V_W + 2 * KIB)
        wt2 = woven_tile("wt2", PACK, AT_WR_DEALT[1])
        weave_wt(nc.scalar.copy, wt1_low[:], 1, 0, 2)
        planes.append(project(2, by_plane))

        wt_q = {}

        def quantise_wt(woven, b, t_from, t_to, home):
            codes, scales = quantise(woven[:], P * (t_to - t_from), "wt%d_%d" % (b, t_from), home)
            for t in range(t_from, t_to):
                wt_q.setdefault((b, t), (codes, scales, P * (t - t_from)))

        x = [pick(0, planes[0])]
        weave_wt(nc.vector.tensor_copy, wt0[:], 0, 0, PACK)
        x.append(pick(1, planes[1]))
        quantise_wt(wt0, 0, 0, PACK, AT_V_W)
        weave_wt(nc.vector.tensor_copy, wt1_high[:], 1, 2, PACK)
        weave_wt(nc.vector.tensor_copy, wt2[:], 2, 0, PACK)
        quantise_wt(wt1_low, 1, 0, 2, None)
        quantise_wt(wt1_high, 1, 2, PACK, None)
        quantise_wt(wt2, 2, 0, PACK, None)
        x.append(pick(2, planes[2]))
        nc.scalar.mul(halved[:], ends[:, :, 0:TYPE_TILES], 0.5)

        def magnitudes(b, lo, width, first_bank):
            size = staged.tile([P, PACK, width], F32, name="size%d_%d" % (b, lo), offset=AT_SIZE[b, lo])
            per_bank = BANK // width
            for k in range(PACK // per_bank):
                acc = psum.tile([P, per_bank, width], F32, name="angle", tag="bank%d" % (first_bank + k))
                for t in range(per_bank * k, per_bank * (k + 1)):
                    codes, scales, col = wt_q[b, t]
                    cols = slice(col, col + P)
                    nc.tensor.matmul_mx(
                        out=acc[:, t % per_bank, :], lhsT=codes[:, cols].bitcast(FP8X4), lhsT_scale=scales[:, cols],
                        rhs=tf_q[0][:, lo : lo + width].bitcast(FP8X4), rhs_scale=tf_q[1][:, lo : lo + width],
                        start=True, stop=True)
                for t in range(per_bank * k, per_bank * (k + 1)):
                    nc.scalar.activation(out=size[:, t, :], in_=acc[:, t % per_bank, :], func=ACT.Abs,
                                         bias=phase_sb[:, b, t : t + 1])
            return size

        def cosine(b, size, lo, width):
            values = keep.tile([P, PACK, width], F32, name="cos%d_%d" % (b, lo))
            nc.scalar.activation(out=values[:], in_=size, func=ACT.Sin, bias=half_pi[:], scale=-1.0)
            return values

        size_first = magnitudes(0, 0, M, 0)
        cos = {(0, 0): cosine(0, size_first[:, :, 0:HALF], 0, HALF)}
        cos[1, 0] = cosine(1, magnitudes(1, 0, HALF, 4)[:], 0, HALF)
        cos[2, 0] = cosine(2, magnitudes(2, 0, HALF, 6)[:], 0, HALF)
        cos[0, HALF] = cosine(0, size_first[:, :, HALF:M], HALF, HALF)
        cos[1, HALF] = cosine(1, magnitudes(1, HALF, HALF, 0)[:], HALF, HALF)
        size_last = magnitudes(2, HALF, HALF, 2)
        cos[2, HALF] = cosine(2, size_last[:, :, 0:QUARTER], HALF, QUARTER)
        cos[2, HALF + QUARTER] = cosine(2, size_last[:, :, QUARTER:HALF], HALF + QUARTER, QUARTER)

        steps = [(b, 0, HALF) for b in range(GROUPS)] + [(b, HALF, HALF) for b in range(LAST)]
        steps = steps + [(LAST, lo, width) for lo, width in PIECES[1:]]
        freed_by = {(1, 0): AT_SIZE[1, 0], (2, 0): AT_SIZE[2, 0], (0, HALF): AT_SIZE[0, 0],
                    (1, HALF): AT_SIZE[1, HALF], (2, HALF + QUARTER): AT_SIZE[2, HALF]}
        z_q = {}
        z_woven = [modulate(*steps[0])]
        for i, (b, lo, width) in enumerate(steps):
            home = None
            if i + 1 < len(steps):
                z_woven.append(modulate(*steps[i + 1]))
                home = freed_by.get(steps[i + 1][0:2])
            z_q[b, lo] = quantise(z_woven[i][:], width, "z%d_%d" % (b, lo), home)

        out_v = out.rearrange("(u p) m -> p u m", p=P)

        for piece, (lo, width) in enumerate(PIECES):
            sums, opens, closes = [], [], []
            for bank, count in SUM_BANKS[piece]:
                acc = psum.tile([P, count, width], F32, name="y%d_%d" % (piece, bank), tag="bank%d" % bank)
                sums.extend(acc[:, i, :] for i in range(count))
                opens.extend(i == 0 for i in range(count))
                closes.extend(i == count - 1 for i in range(count))
            for b in range(GROUPS):
                z_lo = lo if (b, lo) in z_q else HALF
                codes, scales = z_q[b, z_lo]
                within = slice(lo - z_lo, lo - z_lo + width)
                for u in range(TYPE_TILES):
                    nc.tensor.matmul_mx(
                        out=sums[u], lhsT=wf_w[:, b, P * u : P * (u + 1)].bitcast(FP8X4),
                        lhsT_scale=wf_s[:, b, P * u : P * (u + 1)],
                        rhs=codes[:, within].bitcast(FP8X4), rhs_scale=scales[:, within],
                        start=(b == 0 and opens[u]), stop=(b == LAST and closes[u]))
            if piece == 0:
                tanh = staged.tile([P, TYPE_TILES, width], F32, name="tanh0", offset=AT_SIZE[2, HALF] + 4 * QUARTER)
            else:
                tanh = keep.tile([P, TYPE_TILES, width], F32, name="tanh%d" % piece)
            for u_first, tiles in STORES[piece]:
                res = keep.tile([P, tiles, width], F32, name="res%d_%d" % (piece, u_first))
                for u in range(u_first, u_first + tiles):
                    nc.scalar.activation(out=tanh[:, u, :], in_=sums[u], func=ACT.Tanh,
                                         bias=half_bf[:, u : u + 1], scale=0.5)
                    nc.vector.tensor_scalar(res[:, u - u_first, :], tanh[:, u, :], half_sev[:, u : u + 1],
                                            half_sev[:, u : u + 1], ALU.mult, ALU.add)
                nc.sync.dma_start(out_v[:, u_first : u_first + tiles, lo : lo + width], res[:])
